import numpy as np
import ml_dtypes


def mxq(x, axis, fmt="e4m3"):
    dtype, down = {"e4m3": (ml_dtypes.float8_e4m3fn, 7), "e5m2": (ml_dtypes.float8_e5m2, 14)}[fmt]
    v = np.moveaxis(np.asarray(x, np.float32).astype(ml_dtypes.bfloat16).astype(np.float64), axis, -1)
    blocks = v.reshape(v.shape[:-1] + (-1, 32))
    amax = np.abs(blocks).max(-1, keepdims=True)
    byte = np.maximum(np.where(amax > 0, np.frexp(amax)[1] - 1 + 127, 0) - down, 1)
    scale = np.exp2(byte - 127.0)
    codes = (blocks / scale).astype(np.float32).astype(dtype).astype(np.float64)
    return np.moveaxis((codes * scale).reshape(v.shape), -1, axis)


WIDE = False


def mx_kscale(k):
    if not WIDE:
        return np.ones(k)
    levels = np.array([10, -10, 5, -5, 0])
    if k % 512:
        return np.exp2(np.random.permutation(np.resize(levels, k // 32))).repeat(32)
    a = np.empty((k // 512, 16))
    for p in range(k // 512):
        a[p, :8] = np.random.permutation(np.resize(levels, 8))
        for g in range(8):
            far = levels[np.abs(levels - a[p, g]) >= 10]
            a[p, g + 8] = far[np.random.randint(len(far))]
    return np.exp2(a.ravel()).repeat(32)


def f64(x):
    return np.asarray(x).astype(np.float64)


def striped(idx):
    return np.tile(idx.reshape(-1, 16).T, (8, 1)).astype(np.uint16)


def unstriped(offs):
    return offs[:16].T.reshape(-1).astype(np.int64)


def silu(v):
    return v / (1.0 + np.exp(-np.maximum(v, -700.0)))


K, T, D, S, V, H, N = 1024, 1024, 2, 512, 256, 1024, 512


def setup_inputs():
    n = np.random.standard_normal
    s = mx_kscale(K)[:, None]
    u = mx_kscale(H)
    return {
        "xT": (n((K, T)) * s).astype(np.float32),
        "w1": (n((K, H)) / np.sqrt(K) / s * u).astype(np.float32),
        "w2": (n((H, N)) / np.sqrt(H) / u[:, None]).astype(np.float32),
        "gate": np.tile(np.random.uniform(0.2, 1.0, (D, 1, V)) / np.sqrt(D), (1, N, 1)).astype(np.float32),
        "offs": striped(np.random.permutation(T)[:S]),
        "pos1": striped(np.random.permutation(S)[:V]),
        "pos2": striped(np.random.permutation(S)[:V]),
    }


def reference(xT, w1, w2, gate, offs, pos1, pos2):
    idx = unstriped(offs)
    xq = mxq(f64(xT)[:, idx], 0, "e4m3")
    h = silu(mxq(f64(w1), 0, "e4m3").T @ xq)
    y = mxq(f64(w2), 0, "e4m3").T @ mxq(h, 0, "e4m3")
    return sum(f64(gate[d]) * y[:, unstriped(p)] for d, p in enumerate((pos1, pos2)))

@@ -1,0 +1,207 @@
+from contextlib import ExitStack
+
+import concourse.mybir as mybir
+
+K, T, S, H, N, V, D = 1024, 1024, 512, 1024, 512, 256, 2
+FLOPS = 2 * S * (K * H + H * N)
+
+F32 = mybir.dt.float32
+BF16 = mybir.dt.bfloat16
+U32 = mybir.dt.uint32
+U16 = mybir.dt.uint16
+U8 = mybir.dt.uint8
+FP8X4 = mybir.dt.float8_e4m3fn_x4
+COPY = mybir.ActivationFunctionType.Copy
+SILU = mybir.ActivationFunctionType.Silu
+MULT = mybir.AluOpType.mult
+ADD = mybir.AluOpType.add
+
+P = 128
+PACK = 4
+PASS = P * PACK
+PASSES = K // PASS
+NB = S // P
+
+X_SCALAR = {(0, 0): 384, (0, 1): 512, (1, 0): 768, (1, 1): 704}
+W1_SCALAR = {(0, 0): (80,), (0, 1): (40,), (1, 0): (48,), (1, 1): (16, 4)}
+H_BLOCKS = (4, 1)
+W2_SCALAR = {(0, 0): 0, (0, 1): 24, (1, 0): 0, (1, 1): 64}
+
+
+def tile_picked_sub_mlp_silu_sub_e_kernel(
+    tc, xT, w1, w2, gate, offs, pos1, pos2, out
+):
+    nc = tc.nc
+    with ExitStack() as ctx:
+        keep = ctx.enter_context(tc.tile_pool(name="keep", bufs=1))
+        banks = ctx.enter_context(tc.psum_pool(name="banks", bufs=1))
+
+        def held(shape, dtype, name):
+            return keep.tile(shape, dtype, name=name, align_bytes=64)
+
+        offs_t = keep.tile([P, S // 16], U16, name="offs_t")
+        pos_t = [keep.tile([P, V // 16], U16, name=f"pos_t{d}") for d in range(D)]
+        x_raw = {}
+        for s in range(PASSES):
+            for u in range(2):
+                x_raw[s, u] = held([P, 2, T], F32, f"x_raw{s}{u}")
+                rows = xT[s * PASS : (s + 1) * PASS, :].rearrange("(p j) c -> p j c", j=PACK)
+                nc.sync.dma_start(out=x_raw[s, u][:], in_=rows[:, 2 * u : 2 * u + 2, :])
+                if s == 0 and u == 0:
+                    nc.sync.dma_start(offs_t[:], offs)
+        w1_raw = {}
+        rows = w1[:PASS, :].rearrange("(p j) c -> p j c", j=PACK)
+        raw = held([P, PACK, H], F32, "w1_raw0")
+        nc.sync.dma_start(out=raw[:], in_=rows)
+        for b in range(H // PASS):
+            w1_raw[b, 0] = [raw[:, :, b * PASS : (b + 1) * PASS]]
+        rows = w1[PASS:, :].rearrange("(p j) c -> p j c", j=PACK)
+        for b, width in ((0, PASS), (1, PASS // 2)):
+            w1_raw[b, 1] = []
+            for c in range(b * PASS, (b + 1) * PASS, width):
+                raw = held([P, PACK, width], F32, f"w1_raw1{c}")
+                nc.sync.dma_start(out=raw[:], in_=rows[:, :, c : c + width])
+                w1_raw[b, 1].append(raw[:])
+        w2_raw = {}
+        for s in range(PASSES):
+            w2_raw[s] = held([P, PACK, N], F32, f"w2_raw{s}")
+            nc.sync.dma_start(
+                out=w2_raw[s][:], in_=w2[s * PASS : (s + 1) * PASS, :].rearrange("(p j) c -> p j c", j=PACK)
+            )
+        nc.sync.dma_start(pos_t[0][:], pos1)
+        nc.sync.dma_start(pos_t[1][:], pos2)
+        gates = {}
+        for mt in range(N // P):
+            gates[mt] = held([P, D, V], F32, f"gate{mt}")
+            nc.sync.dma_start(
+                out=gates[mt][:], in_=gate[:, mt * P : (mt + 1) * P, :].rearrange("d p v -> p d v")
+            )
+
+        warm = keep.tile([P, 1], F32, name="warm")
+        nc.vector.memset(warm[:], 0.0)
+        nc.scalar.activation(warm[:], warm[:], SILU)
+
+        def quantise(codes, scales, values):
+            nc.vector.quantize_mx(out=codes.bitcast(FP8X4), scales=scales, in_=values)
+
+        def cast(dst, src, cut):
+            if cut:
+                nc.scalar.activation(dst[:, :cut], src[:, :cut], COPY)
+            if cut < src.shape[1]:
+                nc.vector.tensor_copy(dst[:, cut:], src[:, cut:])
+
+        x_codes, x_scales = {}, {}
+        for s in range(PASSES):
+            picked = held([P, S, PACK], BF16, f"picked{s}")
+            words = picked[:].rearrange("p n j -> p (n j)").bitcast(U32).rearrange("p (n u) -> p n u", u=2)
+            for u in range(2):
+                pairs = held([P, T, 2], BF16, f"pairs{s}{u}")
+                src = x_raw[s, u][:].rearrange("p e c -> p c e")
+                cast(pairs, x_raw[s, u][:].rearrange("p e c -> p c e"), X_SCALAR[s, u])
+                window = pairs[:].rearrange("p c e -> p (c e)").bitcast(U32)
+                nc.vector.tensor_copy(words[:, :, u], window.indirect(offs_t[:]))
+            x_codes[s] = held([P, S], U32, f"x_codes{s}")
+            x_scales[s] = held([P, S], U8, f"x_scales{s}")
+            quantise(x_codes[s][:], x_scales[s][:], picked[:].rearrange("p n j -> p (n j)"))
+
+        w1_codes, w1_scales = {}, {}
+
+        def prepare_w1(b, s):
+            grouped = held([P, PACK, P, PACK], BF16, f"w1_grouped{b}{s}")
+            dst = grouped[:].rearrange("p t m j -> p m j t")
+            width = P // len(w1_raw[b, s])
+            for c, raw in enumerate(w1_raw[b, s]):
+                src = raw.rearrange("p j (m t) -> p m j t", t=PACK)
+                cast(dst[:, c * width : (c + 1) * width], src, W1_SCALAR[b, s][c])
+            w1_codes[b, s] = held([P, PASS], U32, f"w1_codes{b}{s}")
+            w1_scales[b, s] = held([P, PASS], U8, f"w1_scales{b}{s}")
+            quantise(w1_codes[b, s][:], w1_scales[b, s][:], grouped[:].rearrange("p t m j -> p (t m j)"))
+
+        h_codes, h_scales = {}, {}
+
+        def product1(b):
+            h = held([P, S, PACK], BF16, f"h{b}")
+            h_codes[b] = held([P, S], U32, f"h_codes{b}")
+            h_scales[b] = held([P, S], U8, f"h_scales{b}")
+            for nb in range(NB):
+                cols = slice(nb * P, (nb + 1) * P)
+                acc = banks.tile([P, PACK, P], F32, name=f"acc{nb}")
+                for s in range(PASSES):
+                    for t in range(PACK):
+                        nc.tensor.matmul_mx(
+                            out=acc[:, t, :],
+                            lhsT=w1_codes[b, s][:, t * P : (t + 1) * P].bitcast(FP8X4),
+                            lhsT_scale=w1_scales[b, s][:, t * P : (t + 1) * P],
+                            rhs=x_codes[s][:, cols].bitcast(FP8X4),
+                            rhs_scale=x_scales[s][:, cols],
+                            start=(s == 0 and t == 0),
+                            stop=(s == PASSES - 1 and t == PACK - 1),
+                        )
+                nc.scalar.activation(h[:, cols, :], acc[:].rearrange("p t n -> p n t"), SILU)
+                if (nb + 1) % H_BLOCKS[b] == 0:
+                    ready = slice((nb + 1 - H_BLOCKS[b]) * P, (nb + 1) * P)
+                    quantise(h_codes[b][:, ready], h_scales[b][:, ready], h[:, ready, :].rearrange("p n t -> p (n t)"))
+
+        prepare_w1(0, 0)
+        prepare_w1(0, 1)
+        prepare_w1(1, 0)
+        product1(0)
+        prepare_w1(1, 1)
+        product1(1)
+
+        y = {}
+        for c in range(2):
+            grouped = held([P, PASSES, N // 2, PACK], BF16, f"w2_grouped{c}")
+            w2_codes = held([P, PASSES, N // 2], U32, f"w2_codes{c}")
+            w2_scales = held([P, PASSES, N // 2], U8, f"w2_scales{c}")
+            for s in range(PASSES):
+                dst = grouped[:, s].rearrange("p (c i) j -> p c j i", i=PACK)
+                src = w2_raw[s][:, :, c * (N // 2) : (c + 1) * (N // 2)].rearrange("p j (c i) -> p c j i", i=PACK)
+                cast(dst, src, W2_SCALAR[s, c])
+                if c == 0:
+                    quantise(w2_codes[:, s], w2_scales[:, s], grouped[:, s].rearrange("p c j -> p (c j)"))
+            if c == 1:
+                quantise(
+                    w2_codes[:].rearrange("p s c -> p (s c)"),
+                    w2_scales[:].rearrange("p s c -> p (s c)"),
+                    grouped[:].rearrange("p s c j -> p (s c j)"),
+                )
+            for mt in (2 * c, 2 * c + 1):
+                total = banks.tile([P, S], F32, name=f"sum{mt}")
+                y[mt] = keep.tile([P, S], F32, name=f"y{mt}")
+                pieces = [slice(nb * P, (nb + 1) * P) for nb in range(NB)] if mt == 0 else [slice(0, S)]
+                for cols in pieces:
+                    for s in range(PASSES):
+                        w_cols = slice(mt % 2 * P, (mt % 2 + 1) * P)
+                        nc.tensor.matmul_mx(
+                            out=total[:, cols],
+                            lhsT=w2_codes[:, s, w_cols].bitcast(FP8X4),
+                            lhsT_scale=w2_scales[:, s, w_cols],
+                            rhs=h_codes[s][:, cols].bitcast(FP8X4),
+                            rhs_scale=h_scales[s][:, cols],
+                            start=(s == 0),
+                            stop=(s == PASSES - 1),
+                        )
+                for cols in (slice(0, S - P), slice(S - P, S)) if mt == 0 else (slice(0, S),):
+                    nc.scalar.activation(y[mt][:, cols], total[:, cols], COPY)
+
+        out_rows = out.rearrange("(m p) v -> p m v", p=P)
+
+        def finish(mts, terms):
+            total = keep.tile([P, len(mts), V], F32, name=f"total{mts[0]}")
+            nc.vector.tensor_tensor(total[:], terms[0][:], terms[1][:], ADD)
+            nc.sync.dma_start(out=out_rows[:, mts[0] : mts[-1] + 1, :], in_=total[:])
+
+        waiting = None
+        for mts in ((0, 1), (2,), (3,)):
+            terms = [keep.tile([P, len(mts), V], F32, name=f"term{mts[0]}{d}") for d in range(D)]
+            for i, mt in enumerate(mts):
+                for d in range(D):
+                    nc.vector.tensor_tensor(
+                        terms[d][:, i, :], y[mt][:].indirect(pos_t[d][:]), gates[mt][:, d, :], MULT
+                    )
+                    if waiting:
+                        finish(*waiting)
+                        waiting = None
+            waiting = (mts, terms)
+        finish(*waiting)

@@ -1,6 +1,7 @@
 from contextlib import ExitStack
 
 import concourse.mybir as mybir
+from concourse.masks import make_identity
 
 K, T, S, H, N, V, D = 1024, 1024, 512, 1024, 512, 256, 2
 FLOPS = 2 * S * (K * H + H * N)
@@ -21,11 +22,28 @@ PACK = 4
 PASS = P * PACK
 PASSES = K // PASS
 NB = S // P
+WARM_PASSES = 4
 
-X_SCALAR = {(0, 0): 384, (0, 1): 512, (1, 0): 768, (1, 1): 704}
-W1_SCALAR = {(0, 0): (80,), (0, 1): (40,), (1, 0): (48,), (1, 1): (16, 4)}
-H_BLOCKS = (4, 1)
-W2_SCALAR = {(0, 0): 0, (0, 1): 24, (1, 0): 0, (1, 1): 64}
+X_SCALAR = {(0, 0): 320, (0, 1): 320, (1, 0): 640, (1, 1): 576}
+W1_SCALAR = {(0, 0): (44,), (1, 0): (60,), (0, 1): (42,), (1, 1): (32, 0)}
+
+PLACES = {
+    "w1_grouped11": 0,
+    "w2_grouped0": 1024,
+    "w2_raw10": 16384,
+    "h_codes01": 16384,
+    "h_codes1": 17408,
+    "w1_raw1768": 6144,
+    "h_codes00": 6144,
+    "h10": 12288,
+    "h11": 13312,
+    "h12": 14336,
+    "h13": 15360,
+    "w2_grouped2": 14336,
+    "terms00": 14336,
+    "w2_grouped3": 12288,
+    "terms11": 12288,
+}
 
 
 def tile_picked_sub_mlp_silu_sub_e_kernel(
@@ -36,50 +54,60 @@ def tile_picked_sub_mlp_silu_sub_e_kernel(
         keep = ctx.enter_context(tc.tile_pool(name="keep", bufs=1))
         banks = ctx.enter_context(tc.psum_pool(name="banks", bufs=1))
 
+        stage = ctx.enter_context(tc.tile_pool(name="stage", bufs=1))
+
         def held(shape, dtype, name):
+            if name in PLACES:
+                return stage.tile(shape, dtype, name=name, align_bytes=64, offset=PLACES[name])
             return keep.tile(shape, dtype, name=name, align_bytes=64)
 
         offs_t = keep.tile([P, S // 16], U16, name="offs_t")
         pos_t = [keep.tile([P, V // 16], U16, name=f"pos_t{d}") for d in range(D)]
-        x_raw = {}
-        for s in range(PASSES):
-            for u in range(2):
-                x_raw[s, u] = held([P, 2, T], F32, f"x_raw{s}{u}")
-                rows = xT[s * PASS : (s + 1) * PASS, :].rearrange("(p j) c -> p j c", j=PACK)
-                nc.sync.dma_start(out=x_raw[s, u][:], in_=rows[:, 2 * u : 2 * u + 2, :])
-                if s == 0 and u == 0:
-                    nc.sync.dma_start(offs_t[:], offs)
-        w1_raw = {}
-        rows = w1[:PASS, :].rearrange("(p j) c -> p j c", j=PACK)
-        raw = held([P, PACK, H], F32, "w1_raw0")
-        nc.sync.dma_start(out=raw[:], in_=rows)
-        for b in range(H // PASS):
-            w1_raw[b, 0] = [raw[:, :, b * PASS : (b + 1) * PASS]]
-        rows = w1[PASS:, :].rearrange("(p j) c -> p j c", j=PACK)
-        for b, width in ((0, PASS), (1, PASS // 2)):
-            w1_raw[b, 1] = []
+        x_raw, w1_raw, w2_raw = {}, {}, {}
+
+        def load_x(s, u):
+            x_raw[s, u] = held([P, 2, T], F32, f"x_raw{s}{u}")
+            rows = xT[s * PASS : (s + 1) * PASS, :].rearrange("(p j) c -> p j c", j=PACK)
+            nc.sync.dma_start(out=x_raw[s, u][:], in_=rows[:, 2 * u : 2 * u + 2, :])
+
+        def load_w1(b, s, width):
+            rows = w1[s * PASS : (s + 1) * PASS, :].rearrange("(p j) c -> p j c", j=PACK)
+            w1_raw[b, s] = []
             for c in range(b * PASS, (b + 1) * PASS, width):
-                raw = held([P, PACK, width], F32, f"w1_raw1{c}")
+                raw = held([P, PACK, width], F32, f"w1_raw{s}{c}")
                 nc.sync.dma_start(out=raw[:], in_=rows[:, :, c : c + width])
-                w1_raw[b, 1].append(raw[:])
-        w2_raw = {}
-        for s in range(PASSES):
-            w2_raw[s] = held([P, PACK, N], F32, f"w2_raw{s}")
-            nc.sync.dma_start(
-                out=w2_raw[s][:], in_=w2[s * PASS : (s + 1) * PASS, :].rearrange("(p j) c -> p j c", j=PACK)
-            )
+                w1_raw[b, s].append(raw[:])
+
+        def load_w2(s, c):
+            w2_raw[s, c] = held([P, PACK, N // 2], F32, f"w2_raw{s}{c}")[:]
+            rows = w2[s * PASS : (s + 1) * PASS, :].rearrange("(p j) c -> p j c", j=PACK)
+            nc.sync.dma_start(out=w2_raw[s, c], in_=rows[:, :, c * (N // 2) : (c + 1) * (N // 2)])
+
+        load_x(0, 0)
+        nc.sync.dma_start(offs_t[:], offs)
+        load_x(0, 1)
+        load_x(1, 0)
+        load_x(1, 1)
+        raw = held([P, PACK, H], F32, "w1_raw0")
+        nc.sync.dma_start(out=raw[:], in_=w1[:PASS, :].rearrange("(p j) c -> p j c", j=PACK))
+        for b in range(2):
+            w1_raw[b, 0] = [raw[:, :, b * PASS : (b + 1) * PASS]]
+        load_w1(0, 1, PASS)
+        load_w1(1, 1, PASS // 2)
+        for c in range(2):
+            for s in range(PASSES):
+                load_w2(s, c)
         nc.sync.dma_start(pos_t[0][:], pos1)
         nc.sync.dma_start(pos_t[1][:], pos2)
-        gates = {}
-        for mt in range(N // P):
-            gates[mt] = held([P, D, V], F32, f"gate{mt}")
-            nc.sync.dma_start(
-                out=gates[mt][:], in_=gate[:, mt * P : (mt + 1) * P, :].rearrange("d p v -> p d v")
-            )
+        gates = held([P, D, V], F32, "gates")
+        nc.sync.dma_start(out=gates[:], in_=gate[:, :P, :].rearrange("d p v -> p d v"))
 
         warm = keep.tile([P, 1], F32, name="warm")
         nc.vector.memset(warm[:], 0.0)
         nc.scalar.activation(warm[:], warm[:], SILU)
+
+        identity = held([P, P], F32, "identity")
+        make_identity(nc, identity[:])
 
         def quantise(codes, scales, values):
             nc.vector.quantize_mx(out=codes.bitcast(FP8X4), scales=scales, in_=values)
@@ -91,12 +119,12 @@ def tile_picked_sub_mlp_silu_sub_e_kernel(
                 nc.vector.tensor_copy(dst[:, cut:], src[:, cut:])
 
         x_codes, x_scales = {}, {}
-        for s in range(PASSES):
+
+        def prepare_x(s):
             picked = held([P, S, PACK], BF16, f"picked{s}")
             words = picked[:].rearrange("p n j -> p (n j)").bitcast(U32).rearrange("p (n u) -> p n u", u=2)
             for u in range(2):
                 pairs = held([P, T, 2], BF16, f"pairs{s}{u}")
-                src = x_raw[s, u][:].rearrange("p e c -> p c e")
                 cast(pairs, x_raw[s, u][:].rearrange("p e c -> p c e"), X_SCALAR[s, u])
                 window = pairs[:].rearrange("p c e -> p (c e)").bitcast(U32)
                 nc.vector.tensor_copy(words[:, :, u], window.indirect(offs_t[:]))
@@ -117,91 +145,170 @@ def tile_picked_sub_mlp_silu_sub_e_kernel(
             w1_scales[b, s] = held([P, PASS], U8, f"w1_scales{b}{s}")
             quantise(w1_codes[b, s][:], w1_scales[b, s][:], grouped[:].rearrange("p t m j -> p (t m j)"))
 
-        h_codes, h_scales = {}, {}
+        acc, h, h_codes, h_scales = {}, {}, {}, {}
 
-        def product1(b):
-            h = held([P, S, PACK], BF16, f"h{b}")
-            h_codes[b] = held([P, S], U32, f"h_codes{b}")
-            h_scales[b] = held([P, S], U8, f"h_scales{b}")
+        def product1(b, s, nb):
+            cols = slice(nb * P, (nb + 1) * P)
+            if s == 0:
+                acc[b, nb] = banks.tile([P, PACK, P], F32, name=f"bank{b * NB + nb}")
+            for t in range(PACK):
+                nc.tensor.matmul_mx(
+                    out=acc[b, nb][:, t, :],
+                    lhsT=w1_codes[b, s][:, t * P : (t + 1) * P].bitcast(FP8X4),
+                    lhsT_scale=w1_scales[b, s][:, t * P : (t + 1) * P],
+                    rhs=x_codes[s][:, cols].bitcast(FP8X4),
+                    rhs_scale=x_scales[s][:, cols],
+                    start=(s == 0 and t == 0),
+                    stop=(s == PASSES - 1 and t == PACK - 1),
+                )
+
+        def hidden(b):
+            if b == 0:
+                whole = held([P, S, PACK], BF16, f"w1_raw1{PASS}")
+                h[b] = [whole[:, nb * P : (nb + 1) * P, :] for nb in range(NB)] + [whole[:]]
+            else:
+                h[b] = [held([P, P, PACK], BF16, f"h1{nb}")[:] for nb in range(NB)]
             for nb in range(NB):
-                cols = slice(nb * P, (nb + 1) * P)
-                acc = banks.tile([P, PACK, P], F32, name=f"acc{nb}")
-                for s in range(PASSES):
-                    for t in range(PACK):
-                        nc.tensor.matmul_mx(
-                            out=acc[:, t, :],
-                            lhsT=w1_codes[b, s][:, t * P : (t + 1) * P].bitcast(FP8X4),
-                            lhsT_scale=w1_scales[b, s][:, t * P : (t + 1) * P],
-                            rhs=x_codes[s][:, cols].bitcast(FP8X4),
-                            rhs_scale=x_scales[s][:, cols],
-                            start=(s == 0 and t == 0),
-                            stop=(s == PASSES - 1 and t == PACK - 1),
-                        )
-                nc.scalar.activation(h[:, cols, :], acc[:].rearrange("p t n -> p n t"), SILU)
-                if (nb + 1) % H_BLOCKS[b] == 0:
-                    ready = slice((nb + 1 - H_BLOCKS[b]) * P, (nb + 1) * P)
-                    quantise(h_codes[b][:, ready], h_scales[b][:, ready], h[:, ready, :].rearrange("p n t -> p (n t)"))
+                product1(b, PASSES - 1, nb)
+                nc.scalar.activation(h[b][nb], acc[b, nb][:].rearrange("p t n -> p n t"), SILU)
 
+        prepare_x(0)
+        prepare_x(1)
+        idle = banks.tile([P, S], F32, name=f"bank{2 * NB - 1}")
+        for i in range(WARM_PASSES):
+            nc.tensor.matmul_mx(
+                out=idle[:],
+                lhsT=x_codes[1][:, :P].bitcast(FP8X4),
+                lhsT_scale=x_scales[1][:, :P],
+                rhs=x_codes[1][:].bitcast(FP8X4),
+                rhs_scale=x_scales[1][:],
+                start=True,
+                stop=True,
+            )
         prepare_w1(0, 0)
+        for nb in range(NB):
+            product1(0, 0, nb)
         prepare_w1(0, 1)
         prepare_w1(1, 0)
-        product1(0)
+        hidden(0)
+        for nb in range(NB):
+            product1(1, 0, nb)
         prepare_w1(1, 1)
-        product1(1)
+        hidden(1)
+        for b in range(2):
+            h_scales[b] = held([P, S], U8, f"h_scales{b}")
 
-        y = {}
-        for c in range(2):
-            grouped = held([P, PASSES, N // 2, PACK], BF16, f"w2_grouped{c}")
-            w2_codes = held([P, PASSES, N // 2], U32, f"w2_codes{c}")
-            w2_scales = held([P, PASSES, N // 2], U8, f"w2_scales{c}")
+        def quantise_h0(half):
+            cols = slice(half * S // 2, (half + 1) * S // 2)
+            h_codes[0, half] = held([P, S // 2], U32, f"h_codes0{half}")
+            quantise(h_codes[0, half][:], h_scales[0][:, cols], h[0][NB][:, cols, :].rearrange("p n t -> p (n t)"))
+
+        def quantise_h1():
+            h_codes[1] = held([P, S], U32, "h_codes1")
+            for nb in range(NB):
+                cols = slice(nb * P, (nb + 1) * P)
+                quantise(h_codes[1][:, cols], h_scales[1][:, cols], h[1][nb].rearrange("p n t -> p (n t)"))
+
+        def h_words(s, cols):
+            if s == 1:
+                return h_codes[1][:, cols]
+            half = cols.start // (S // 2)
+            return h_codes[0, half][:, cols.start - half * S // 2 : cols.stop - half * S // 2]
+
+        y, w2_codes, w2_scales = {}, {}, {}
+
+        def prepare_w2(first, tiles):
+            width = tiles * P
+            grouped = held([P, PASSES, width, PACK], BF16, f"w2_grouped{first}")
+            codes = held([P, PASSES, width], U32, f"w2_codes{first}")
+            scales = held([P, PASSES, width], U8, f"w2_scales{first}")
             for s in range(PASSES):
                 dst = grouped[:, s].rearrange("p (c i) j -> p c j i", i=PACK)
-                src = w2_raw[s][:, :, c * (N // 2) : (c + 1) * (N // 2)].rearrange("p j (c i) -> p c j i", i=PACK)
-                cast(dst, src, W2_SCALAR[s, c])
-                if c == 0:
-                    quantise(w2_codes[:, s], w2_scales[:, s], grouped[:, s].rearrange("p c j -> p (c j)"))
-            if c == 1:
-                quantise(
-                    w2_codes[:].rearrange("p s c -> p (s c)"),
-                    w2_scales[:].rearrange("p s c -> p (s c)"),
-                    grouped[:].rearrange("p s c j -> p (s c j)"),
+                src = w2_raw[s, first // 2][:, :, first % 2 * P : first % 2 * P + width]
+                cast(dst, src.rearrange("p j (c i) -> p c j i", i=PACK), width // PACK if first == 3 else 0)
+            quantise(
+                codes[:].rearrange("p s c -> p (s c)"),
+                scales[:].rearrange("p s c -> p (s c)"),
+                grouped[:].rearrange("p s c j -> p (s c j)"),
+            )
+            for i in range(tiles):
+                w2_codes[first + i] = codes[:, :, i * P : (i + 1) * P]
+                w2_scales[first + i] = scales[:, :, i * P : (i + 1) * P]
+
+        def product2(mt):
+            total = banks.tile([P, S], F32, name=f"bank{mt}")
+            y[mt] = held([P, S], F32, "w2_raw11" if mt == 2 else f"y{mt}")
+            if mt == 0:
+                steps = [(s, slice(nb * P, (nb + 1) * P), s == 0, s == 1) for nb in range(NB) for s in range(PASSES)]
+            else:
+                steps = [(0, slice(0, S // 2), True, False), (0, slice(S // 2, S), False, False), (1, slice(0, S), False, True)]
+            for s, cols, start, stop in steps:
+                nc.tensor.matmul_mx(
+                    out=total[:, cols],
+                    lhsT=w2_codes[mt][:, s].bitcast(FP8X4),
+                    lhsT_scale=w2_scales[mt][:, s],
+                    rhs=h_words(s, cols).bitcast(FP8X4),
+                    rhs_scale=h_scales[s][:, cols],
+                    start=start,
+                    stop=stop,
                 )
-            for mt in (2 * c, 2 * c + 1):
-                total = banks.tile([P, S], F32, name=f"sum{mt}")
-                y[mt] = keep.tile([P, S], F32, name=f"y{mt}")
-                pieces = [slice(nb * P, (nb + 1) * P) for nb in range(NB)] if mt == 0 else [slice(0, S)]
-                for cols in pieces:
-                    for s in range(PASSES):
-                        w_cols = slice(mt % 2 * P, (mt % 2 + 1) * P)
-                        nc.tensor.matmul_mx(
-                            out=total[:, cols],
-                            lhsT=w2_codes[:, s, w_cols].bitcast(FP8X4),
-                            lhsT_scale=w2_scales[:, s, w_cols],
-                            rhs=h_codes[s][:, cols].bitcast(FP8X4),
-                            rhs_scale=h_scales[s][:, cols],
-                            start=(s == 0),
-                            stop=(s == PASSES - 1),
-                        )
-                for cols in (slice(0, S - P), slice(S - P, S)) if mt == 0 else (slice(0, S),):
+            if mt == 0:
+                for cols in (slice(0, S - P), slice(S - P, S)):
                     nc.scalar.activation(y[mt][:, cols], total[:, cols], COPY)
+            else:
+                nc.scalar.activation(y[mt][:], total[:], COPY)
+
+        quantise_h0(0)
+        quantise_h0(1)
+        prepare_w2(0, 2)
+        quantise_h1()
+        product2(0)
+        prepare_w2(2, 1)
+        product2(1)
+        prepare_w2(3, 1)
+        product2(2)
+        product2(3)
 
         out_rows = out.rearrange("(m p) v -> p m v", p=P)
 
-        def finish(mts, terms):
-            total = keep.tile([P, len(mts), V], F32, name=f"total{mts[0]}")
-            nc.vector.tensor_tensor(total[:], terms[0][:], terms[1][:], ADD)
-            nc.sync.dma_start(out=out_rows[:, mts[0] : mts[-1] + 1, :], in_=total[:])
-
-        waiting = None
-        for mts in ((0, 1), (2,), (3,)):
-            terms = [keep.tile([P, len(mts), V], F32, name=f"term{mts[0]}{d}") for d in range(D)]
-            for i, mt in enumerate(mts):
+        def finish_by_transposes(mt, terms):
+            turned = banks.tile([P, V], F32, name=f"bank{2 + mt}")
+            for vb in range(V // P):
+                cols = slice(vb * P, (vb + 1) * P)
                 for d in range(D):
-                    nc.vector.tensor_tensor(
-                        terms[d][:, i, :], y[mt][:].indirect(pos_t[d][:]), gates[mt][:, d, :], MULT
+                    nc.tensor.matmul(
+                        turned[:, cols], terms[d][:, cols], identity[:], start=(d == 0), stop=(d == D - 1), is_transpose=True
                     )
-                    if waiting:
-                        finish(*waiting)
-                        waiting = None
-            waiting = (mts, terms)
-        finish(*waiting)
+            summed = held([P, V], F32, f"summed{mt}")
+            nc.scalar.activation(summed[:], turned[:], COPY)
+            back = banks.tile([P, V], F32, name=f"bank{NB + mt}")
+            for vb in range(V // P):
+                cols = slice(vb * P, (vb + 1) * P)
+                nc.tensor.transpose(back[:, cols], summed[:, cols], identity[:])
+            total = held([P, V], F32, f"total{mt}")
+            nc.scalar.activation(total[:], back[:], COPY)
+            nc.scalar.dma_start(out=out_rows[:, mt, :], in_=total[:])
+
+        def finish(mt, terms):
+            if mt < 2:
+                finish_by_transposes(mt, terms)
+                return
+            total = keep.tile([P, V], F32, name=f"total{mt}")
+            nc.vector.tensor_tensor(total[:], terms[0][:], terms[1][:], ADD)
+            nc.sync.dma_start(out=out_rows[:, mt, :], in_=total[:])
+
+        terms = {}
+
+        def fetch(mt, d):
+            terms[mt, d] = held([P, V], F32, f"terms{mt}{d}")
+            nc.vector.tensor_tensor(terms[mt, d][:], y[mt][:].indirect(pos_t[d][:]), gates[:, d, :], MULT)
+
+        for mt in range(2):
+            for d in range(D):
+                fetch(mt, d)
+            finish(mt, [terms[mt, d] for d in range(D)])
+        for d in range(D):
+            for mt in range(2, 4):
+                fetch(mt, d)
+        for mt in range(2, 4):
+            finish(mt, [terms[mt, d] for d in range(D)])

@@ -21,28 +21,32 @@ P = 128
 PACK = 4
 PASS = P * PACK
 PASSES = K // PASS
-NB = S // P
-WARM_PASSES = 4
+BLOCKS = S // P
+TILES = N // P
+HALF = S // 2
 
 X_SCALAR = {(0, 0): 320, (0, 1): 320, (1, 0): 640, (1, 1): 576}
-W1_SCALAR = {(0, 0): (44,), (1, 0): (60,), (0, 1): (42,), (1, 1): (32, 0)}
+W1_SCALAR = {(0, 0): 44, (1, 0): 60, (0, 1): 42}
+W1_SHORT = 24
+WARM_PASSES = 4
 
-PLACES = {
-    "w1_grouped11": 0,
+TURNS = {
+    "w1_grouped111": 0,
+    "h_codes00": 0,
     "w2_grouped0": 1024,
-    "w2_raw10": 16384,
-    "h_codes01": 16384,
-    "h_codes1": 17408,
-    "w1_raw1768": 6144,
-    "h_codes00": 6144,
     "h10": 12288,
     "h11": 13312,
+    "w2_grouped3": 12288,
+    "terms11": 12288,
     "h12": 14336,
     "h13": 15360,
     "w2_grouped2": 14336,
     "terms00": 14336,
-    "w2_grouped3": 12288,
-    "terms11": 12288,
+    "w2_raw10": 16384,
+    "h_codes01": 16384,
+    "h_codes1": 17408,
+    "w1_grouped010": 24576,
+    "w1_scales10": 24576,
 }
 
 
@@ -53,50 +57,39 @@ def tile_picked_sub_mlp_silu_sub_e_kernel(
     with ExitStack() as ctx:
         keep = ctx.enter_context(tc.tile_pool(name="keep", bufs=1))
         banks = ctx.enter_context(tc.psum_pool(name="banks", bufs=1))
-
-        stage = ctx.enter_context(tc.tile_pool(name="stage", bufs=1))
+        turns = ctx.enter_context(tc.tile_pool(name="turns", bufs=1))
 
         def held(shape, dtype, name):
-            if name in PLACES:
-                return stage.tile(shape, dtype, name=name, align_bytes=64, offset=PLACES[name])
+            if name in TURNS:
+                return turns.tile(shape, dtype, name=name, align_bytes=64, offset=TURNS[name])
             return keep.tile(shape, dtype, name=name, align_bytes=64)
+
+        def pass_rows(matrix, s):
+            return matrix[s * PASS : (s + 1) * PASS, :].rearrange("(p j) c -> p j c", j=PACK)
 
         offs_t = keep.tile([P, S // 16], U16, name="offs_t")
         pos_t = [keep.tile([P, V // 16], U16, name=f"pos_t{d}") for d in range(D)]
         x_raw, w1_raw, w2_raw = {}, {}, {}
 
-        def load_x(s, u):
-            x_raw[s, u] = held([P, 2, T], F32, f"x_raw{s}{u}")
-            rows = xT[s * PASS : (s + 1) * PASS, :].rearrange("(p j) c -> p j c", j=PACK)
-            nc.sync.dma_start(out=x_raw[s, u][:], in_=rows[:, 2 * u : 2 * u + 2, :])
+        def load(matrix, s, first, width, name):
+            raw = held([P, PACK, width], F32, name)
+            nc.sync.dma_start(out=raw[:], in_=pass_rows(matrix, s)[:, :, first : first + width])
+            return raw[:]
 
-        def load_w1(b, s, width):
-            rows = w1[s * PASS : (s + 1) * PASS, :].rearrange("(p j) c -> p j c", j=PACK)
-            w1_raw[b, s] = []
-            for c in range(b * PASS, (b + 1) * PASS, width):
-                raw = held([P, PACK, width], F32, f"w1_raw{s}{c}")
-                nc.sync.dma_start(out=raw[:], in_=rows[:, :, c : c + width])
-                w1_raw[b, s].append(raw[:])
-
-        def load_w2(s, c):
-            w2_raw[s, c] = held([P, PACK, N // 2], F32, f"w2_raw{s}{c}")[:]
-            rows = w2[s * PASS : (s + 1) * PASS, :].rearrange("(p j) c -> p j c", j=PACK)
-            nc.sync.dma_start(out=w2_raw[s, c], in_=rows[:, :, c * (N // 2) : (c + 1) * (N // 2)])
-
-        load_x(0, 0)
-        nc.sync.dma_start(offs_t[:], offs)
-        load_x(0, 1)
-        load_x(1, 0)
-        load_x(1, 1)
-        raw = held([P, PACK, H], F32, "w1_raw0")
-        nc.sync.dma_start(out=raw[:], in_=w1[:PASS, :].rearrange("(p j) c -> p j c", j=PACK))
+        for s in range(PASSES):
+            for u in range(2):
+                x_raw[s, u] = held([P, 2, T], F32, f"x_raw{s}{u}")
+                nc.sync.dma_start(out=x_raw[s, u][:], in_=pass_rows(xT, s)[:, 2 * u : 2 * u + 2, :])
+                if (s, u) == (0, 0):
+                    nc.sync.dma_start(offs_t[:], offs)
+        whole = load(w1, 0, 0, H, "w1_raw0")
         for b in range(2):
-            w1_raw[b, 0] = [raw[:, :, b * PASS : (b + 1) * PASS]]
-        load_w1(0, 1, PASS)
-        load_w1(1, 1, PASS // 2)
+            w1_raw[b, 0] = [whole[:, :, b * PASS : (b + 1) * PASS]]
+        w1_raw[0, 1] = [load(w1, 1, 0, PASS, "w1_raw01")]
+        w1_raw[1, 1] = [load(w1, 1, PASS + c * PASS // 2, PASS // 2, f"w1_raw11{c}") for c in range(2)]
         for c in range(2):
             for s in range(PASSES):
-                load_w2(s, c)
+                w2_raw[s, c] = load(w2, s, c * N // 2, N // 2, f"w2_raw{s}{c}")
         nc.sync.dma_start(pos_t[0][:], pos1)
         nc.sync.dma_start(pos_t[1][:], pos2)
         gates = held([P, D, V], F32, "gates")
@@ -118,9 +111,19 @@ def tile_picked_sub_mlp_silu_sub_e_kernel(
             if cut < src.shape[1]:
                 nc.vector.tensor_copy(dst[:, cut:], src[:, cut:])
 
-        x_codes, x_scales = {}, {}
+        def multiply(result, stationary, moving, start, stop):
+            nc.tensor.matmul_mx(
+                out=result,
+                lhsT=stationary[0].bitcast(FP8X4),
+                lhsT_scale=stationary[1],
+                rhs=moving[0].bitcast(FP8X4),
+                rhs_scale=moving[1],
+                start=start,
+                stop=stop,
+            )
 
-        def prepare_x(s):
+        x_codes, x_scales = {}, {}
+        for s in range(PASSES):
             picked = held([P, S, PACK], BF16, f"picked{s}")
             words = picked[:].rearrange("p n j -> p (n j)").bitcast(U32).rearrange("p (n u) -> p n u", u=2)
             for u in range(2):
@@ -132,183 +135,173 @@ def tile_picked_sub_mlp_silu_sub_e_kernel(
             x_scales[s] = held([P, S], U8, f"x_scales{s}")
             quantise(x_codes[s][:], x_scales[s][:], picked[:].rearrange("p n j -> p (n j)"))
 
+        idle = banks.tile([P, S], F32, name=f"bank{2 * BLOCKS - 1}")
+        for i in range(WARM_PASSES):
+            multiply(idle[:], (x_codes[1][:, :P], x_scales[1][:, :P]), (x_codes[1][:], x_scales[1][:]), True, True)
+
         w1_codes, w1_scales = {}, {}
 
-        def prepare_w1(b, s):
-            grouped = held([P, PACK, P, PACK], BF16, f"w1_grouped{b}{s}")
-            dst = grouped[:].rearrange("p t m j -> p m j t")
+        def prepare_w1(b, s, tiles_at_once):
+            w1_codes[b, s] = held([P, PACK, P], U32, f"w1_codes{b}{s}")
+            w1_scales[b, s] = held([P, PACK, P], U8, f"w1_scales{b}{s}")
             width = P // len(w1_raw[b, s])
             for c, raw in enumerate(w1_raw[b, s]):
+                grouped = held([P, PACK, width, PACK], BF16, f"w1_grouped{b}{s}{c}")
+                dst = grouped[:].rearrange("p t m j -> p m j t")
                 src = raw.rearrange("p j (m t) -> p m j t", t=PACK)
-                cast(dst[:, c * width : (c + 1) * width], src, W1_SCALAR[b, s][c])
-            w1_codes[b, s] = held([P, PASS], U32, f"w1_codes{b}{s}")
-            w1_scales[b, s] = held([P, PASS], U8, f"w1_scales{b}{s}")
-            quantise(w1_codes[b, s][:], w1_scales[b, s][:], grouped[:].rearrange("p t m j -> p (t m j)"))
+                if (b, s) == (1, 0):
+                    rest = width - W1_SHORT
+                    nc.vector.tensor_copy(dst[:, rest:], src[:, rest:])
+                    cast(dst[:, :rest], src[:, :rest], W1_SCALAR[b, s])
+                elif (b, s) == (1, 1):
+                    cast(dst, src, width if c == 0 else 0)
+                else:
+                    cast(dst, src, W1_SCALAR[b, s])
+                columns = slice(c * width, (c + 1) * width)
+                for t in range(0, PACK, tiles_at_once):
+                    some = slice(t, t + tiles_at_once)
+                    quantise(
+                        w1_codes[b, s][:, some, columns].rearrange("p t m -> p (t m)"),
+                        w1_scales[b, s][:, some, columns].rearrange("p t m -> p (t m)"),
+                        grouped[:, some].rearrange("p t m j -> p (t m j)"),
+                    )
 
-        acc, h, h_codes, h_scales = {}, {}, {}, {}
+        acc, h = {}, {}
 
         def product1(b, s, nb):
-            cols = slice(nb * P, (nb + 1) * P)
+            nodes = slice(nb * P, (nb + 1) * P)
             if s == 0:
-                acc[b, nb] = banks.tile([P, PACK, P], F32, name=f"bank{b * NB + nb}")
+                acc[b, nb] = banks.tile([P, PACK, P], F32, name=f"bank{b * BLOCKS + nb}")
             for t in range(PACK):
-                nc.tensor.matmul_mx(
-                    out=acc[b, nb][:, t, :],
-                    lhsT=w1_codes[b, s][:, t * P : (t + 1) * P].bitcast(FP8X4),
-                    lhsT_scale=w1_scales[b, s][:, t * P : (t + 1) * P],
-                    rhs=x_codes[s][:, cols].bitcast(FP8X4),
-                    rhs_scale=x_scales[s][:, cols],
-                    start=(s == 0 and t == 0),
-                    stop=(s == PASSES - 1 and t == PACK - 1),
+                multiply(
+                    acc[b, nb][:, t, :],
+                    (w1_codes[b, s][:, t, :], w1_scales[b, s][:, t, :]),
+                    (x_codes[s][:, nodes], x_scales[s][:, nodes]),
+                    s == 0 and t == 0,
+                    s == PASSES - 1 and t == PACK - 1,
                 )
 
-        def hidden(b):
-            if b == 0:
-                whole = held([P, S, PACK], BF16, f"w1_raw1{PASS}")
-                h[b] = [whole[:, nb * P : (nb + 1) * P, :] for nb in range(NB)] + [whole[:]]
-            else:
-                h[b] = [held([P, P, PACK], BF16, f"h1{nb}")[:] for nb in range(NB)]
-            for nb in range(NB):
+        def last_pass_and_silu(b):
+            for nb in range(BLOCKS):
                 product1(b, PASSES - 1, nb)
-                nc.scalar.activation(h[b][nb], acc[b, nb][:].rearrange("p t n -> p n t"), SILU)
+                nc.scalar.activation(h[b, nb], acc[b, nb][:].rearrange("p t n -> p n t"), SILU)
 
-        prepare_x(0)
-        prepare_x(1)
-        idle = banks.tile([P, S], F32, name=f"bank{2 * NB - 1}")
-        for i in range(WARM_PASSES):
-            nc.tensor.matmul_mx(
-                out=idle[:],
-                lhsT=x_codes[1][:, :P].bitcast(FP8X4),
-                lhsT_scale=x_scales[1][:, :P],
-                rhs=x_codes[1][:].bitcast(FP8X4),
-                rhs_scale=x_scales[1][:],
-                start=True,
-                stop=True,
-            )
-        prepare_w1(0, 0)
-        for nb in range(NB):
+        prepare_w1(0, 0, PACK)
+        for nb in range(BLOCKS):
             product1(0, 0, nb)
-        prepare_w1(0, 1)
-        prepare_w1(1, 0)
-        hidden(0)
-        for nb in range(NB):
+        prepare_w1(0, 1, 2)
+        prepare_w1(1, 0, PACK)
+        h_first = held([P, S, PACK], BF16, "w1_raw110")
+        for nb in range(BLOCKS):
+            h[0, nb] = h_first[:, nb * P : (nb + 1) * P, :]
+        last_pass_and_silu(0)
+        for nb in range(BLOCKS):
             product1(1, 0, nb)
-        prepare_w1(1, 1)
-        hidden(1)
-        for b in range(2):
-            h_scales[b] = held([P, S], U8, f"h_scales{b}")
+        prepare_w1(1, 1, 1)
+        for nb in range(BLOCKS):
+            h[1, nb] = held([P, P, PACK], BF16, f"h1{nb}")[:]
+        last_pass_and_silu(1)
 
-        def quantise_h0(half):
-            cols = slice(half * S // 2, (half + 1) * S // 2)
-            h_codes[0, half] = held([P, S // 2], U32, f"h_codes0{half}")
-            quantise(h_codes[0, half][:], h_scales[0][:, cols], h[0][NB][:, cols, :].rearrange("p n t -> p (n t)"))
+        h_scales = [held([P, S], U8, f"h_scales{s}") for s in range(PASSES)]
+        h_codes_first = []
+        for half in range(2):
+            nodes = slice(half * HALF, (half + 1) * HALF)
+            h_codes_first.append(held([P, HALF], U32, f"h_codes0{half}"))
+            quantise(h_codes_first[half][:], h_scales[0][:, nodes], h_first[:, nodes, :].rearrange("p n t -> p (n t)"))
 
-        def quantise_h1():
-            h_codes[1] = held([P, S], U32, "h_codes1")
-            for nb in range(NB):
-                cols = slice(nb * P, (nb + 1) * P)
-                quantise(h_codes[1][:, cols], h_scales[1][:, cols], h[1][nb].rearrange("p n t -> p (n t)"))
+        w2_codes, w2_scales = {}, {}
 
-        def h_words(s, cols):
-            if s == 1:
-                return h_codes[1][:, cols]
-            half = cols.start // (S // 2)
-            return h_codes[0, half][:, cols.start - half * S // 2 : cols.stop - half * S // 2]
-
-        y, w2_codes, w2_scales = {}, {}, {}
-
-        def prepare_w2(first, tiles):
-            width = tiles * P
+        def prepare_w2(first, count, on_scalar):
+            width = count * P
             grouped = held([P, PASSES, width, PACK], BF16, f"w2_grouped{first}")
             codes = held([P, PASSES, width], U32, f"w2_codes{first}")
             scales = held([P, PASSES, width], U8, f"w2_scales{first}")
             for s in range(PASSES):
                 dst = grouped[:, s].rearrange("p (c i) j -> p c j i", i=PACK)
                 src = w2_raw[s, first // 2][:, :, first % 2 * P : first % 2 * P + width]
-                cast(dst, src.rearrange("p j (c i) -> p c j i", i=PACK), width // PACK if first == 3 else 0)
+                cast(dst, src.rearrange("p j (c i) -> p c j i", i=PACK), width // PACK if on_scalar else 0)
             quantise(
                 codes[:].rearrange("p s c -> p (s c)"),
                 scales[:].rearrange("p s c -> p (s c)"),
                 grouped[:].rearrange("p s c j -> p (s c j)"),
             )
-            for i in range(tiles):
+            for i in range(count):
                 w2_codes[first + i] = codes[:, :, i * P : (i + 1) * P]
                 w2_scales[first + i] = scales[:, :, i * P : (i + 1) * P]
+
+        prepare_w2(0, 2, False)
+        h_codes_second = held([P, S], U32, "h_codes1")
+        for nb in range(BLOCKS):
+            nodes = slice(nb * P, (nb + 1) * P)
+            quantise(h_codes_second[:, nodes], h_scales[1][:, nodes], h[1, nb].rearrange("p n t -> p (n t)"))
+
+        def h_operand(s, nodes):
+            if s == 1:
+                return h_codes_second[:, nodes], h_scales[1][:, nodes]
+            half = nodes.start // HALF
+            return h_codes_first[half][:, nodes.start - half * HALF : nodes.stop - half * HALF], h_scales[0][:, nodes]
+
+        y = {}
 
         def product2(mt):
             total = banks.tile([P, S], F32, name=f"bank{mt}")
             y[mt] = held([P, S], F32, "w2_raw11" if mt == 2 else f"y{mt}")
             if mt == 0:
-                steps = [(s, slice(nb * P, (nb + 1) * P), s == 0, s == 1) for nb in range(NB) for s in range(PASSES)]
+                steps = [(s, slice(nb * P, (nb + 1) * P), s == 0, s == 1) for nb in range(BLOCKS) for s in range(PASSES)]
+                copies = [slice(0, S - P), slice(S - P, S)]
             else:
-                steps = [(0, slice(0, S // 2), True, False), (0, slice(S // 2, S), False, False), (1, slice(0, S), False, True)]
-            for s, cols, start, stop in steps:
-                nc.tensor.matmul_mx(
-                    out=total[:, cols],
-                    lhsT=w2_codes[mt][:, s].bitcast(FP8X4),
-                    lhsT_scale=w2_scales[mt][:, s],
-                    rhs=h_words(s, cols).bitcast(FP8X4),
-                    rhs_scale=h_scales[s][:, cols],
-                    start=start,
-                    stop=stop,
-                )
-            if mt == 0:
-                for cols in (slice(0, S - P), slice(S - P, S)):
-                    nc.scalar.activation(y[mt][:, cols], total[:, cols], COPY)
-            else:
-                nc.scalar.activation(y[mt][:], total[:], COPY)
+                steps = [(0, slice(0, HALF), True, False), (0, slice(HALF, S), False, False), (1, slice(0, S), False, True)]
+                copies = [slice(0, S)]
+            for s, nodes, start, stop in steps:
+                multiply(total[:, nodes], (w2_codes[mt][:, s], w2_scales[mt][:, s]), h_operand(s, nodes), start, stop)
+            for nodes in copies:
+                nc.scalar.activation(y[mt][:, nodes], total[:, nodes], COPY)
 
-        quantise_h0(0)
-        quantise_h0(1)
-        prepare_w2(0, 2)
-        quantise_h1()
         product2(0)
-        prepare_w2(2, 1)
+        prepare_w2(2, 1, False)
         product2(1)
-        prepare_w2(3, 1)
+        prepare_w2(3, 1, True)
         product2(2)
         product2(3)
 
         out_rows = out.rearrange("(m p) v -> p m v", p=P)
-
-        def finish_by_transposes(mt, terms):
-            turned = banks.tile([P, V], F32, name=f"bank{2 + mt}")
-            for vb in range(V // P):
-                cols = slice(vb * P, (vb + 1) * P)
-                for d in range(D):
-                    nc.tensor.matmul(
-                        turned[:, cols], terms[d][:, cols], identity[:], start=(d == 0), stop=(d == D - 1), is_transpose=True
-                    )
-            summed = held([P, V], F32, f"summed{mt}")
-            nc.scalar.activation(summed[:], turned[:], COPY)
-            back = banks.tile([P, V], F32, name=f"bank{NB + mt}")
-            for vb in range(V // P):
-                cols = slice(vb * P, (vb + 1) * P)
-                nc.tensor.transpose(back[:, cols], summed[:, cols], identity[:])
-            total = held([P, V], F32, f"total{mt}")
-            nc.scalar.activation(total[:], back[:], COPY)
-            nc.scalar.dma_start(out=out_rows[:, mt, :], in_=total[:])
-
-        def finish(mt, terms):
-            if mt < 2:
-                finish_by_transposes(mt, terms)
-                return
-            total = keep.tile([P, V], F32, name=f"total{mt}")
-            nc.vector.tensor_tensor(total[:], terms[0][:], terms[1][:], ADD)
-            nc.sync.dma_start(out=out_rows[:, mt, :], in_=total[:])
-
         terms = {}
 
         def fetch(mt, d):
             terms[mt, d] = held([P, V], F32, f"terms{mt}{d}")
             nc.vector.tensor_tensor(terms[mt, d][:], y[mt][:].indirect(pos_t[d][:]), gates[:, d, :], MULT)
 
-        for mt in range(2):
+        def add_by_transposes(mt):
+            turned = banks.tile([P, V], F32, name=f"bank{mt + 2}")
+            for vb in range(V // P):
+                targets = slice(vb * P, (vb + 1) * P)
+                for d in range(D):
+                    nc.tensor.matmul(
+                        turned[:, targets],
+                        terms[mt, d][:, targets],
+                        identity[:],
+                        start=(d == 0),
+                        stop=(d == D - 1),
+                        is_transpose=True,
+                    )
+            summed = held([P, V], F32, f"summed{mt}")
+            nc.scalar.activation(summed[:], turned[:], COPY)
+            back = banks.tile([P, V], F32, name=f"bank{BLOCKS + mt}")
+            for vb in range(V // P):
+                part = slice(vb * P, (vb + 1) * P)
+                nc.tensor.transpose(back[:, part], summed[:, part], identity[:])
+            result = held([P, V], F32, f"result{mt}")
+            nc.scalar.activation(result[:], back[:], COPY)
+            nc.scalar.dma_start(out=out_rows[:, mt, :], in_=result[:])
+
+        for mt in range(TILES // 2):
             for d in range(D):
                 fetch(mt, d)
-            finish(mt, [terms[mt, d] for d in range(D)])
+            add_by_transposes(mt)
         for d in range(D):
-            for mt in range(2, 4):
+            for mt in range(TILES // 2, TILES):
                 fetch(mt, d)
-        for mt in range(2, 4):
-            finish(mt, [terms[mt, d] for d in range(D)])
+        for mt in range(TILES // 2, TILES):
+            result = keep.tile([P, V], F32, name=f"result{mt}")
+            nc.vector.tensor_tensor(result[:], terms[mt, 0][:], terms[mt, 1][:], ADD)
+            nc.sync.dma_start(out=out_rows[:, mt, :], in_=result[:])

@@ -32,19 +32,21 @@ WARM_PASSES = 4
 
 TURNS = {
     "w1_grouped111": 0,
-    "h_codes00": 0,
-    "w2_grouped0": 1024,
-    "h10": 12288,
-    "h11": 13312,
-    "w2_grouped3": 12288,
-    "terms11": 12288,
-    "h12": 14336,
-    "h13": 15360,
-    "w2_grouped2": 14336,
-    "terms00": 14336,
-    "w2_raw10": 16384,
-    "h_codes01": 16384,
-    "h_codes1": 17408,
+    "h_scales0": 0,
+    "w2_grouped00": 1024,
+    "h13": 4096,
+    "w2_grouped02": 3584,
+    "w2_grouped03": 4608,
+    "w2_raw02": 8192,
+    "w2_grouped12": 8192,
+    "w2_grouped13": 11264,
+    "w2_raw12": 16384,
+    "y1": 16384,
+    "w2_raw13": 20480,
+    "y2": 19456,
+    "summed0": 21504,
+    "gates0": 12288,
+    "result2": 12288,
     "w1_grouped010": 24576,
     "w1_scales10": 24576,
 }
@@ -82,18 +84,23 @@ def tile_picked_sub_mlp_silu_sub_e_kernel(
                 nc.sync.dma_start(out=x_raw[s, u][:], in_=pass_rows(xT, s)[:, 2 * u : 2 * u + 2, :])
                 if (s, u) == (0, 0):
                     nc.sync.dma_start(offs_t[:], offs)
+                    gate_quads = held([P, PACK], F32, "gate_quads")
+                    for d in range(D):
+                        nc.sync.dma_start(
+                            out=gate_quads[d * V // PACK : (d + 1) * V // PACK, :],
+                            in_=gate[d, 0, :].rearrange("(q i) -> q i", i=PACK),
+                        )
         whole = load(w1, 0, 0, H, "w1_raw0")
         for b in range(2):
             w1_raw[b, 0] = [whole[:, :, b * PASS : (b + 1) * PASS]]
         w1_raw[0, 1] = [load(w1, 1, 0, PASS, "w1_raw01")]
         w1_raw[1, 1] = [load(w1, 1, PASS + c * PASS // 2, PASS // 2, f"w1_raw11{c}") for c in range(2)]
-        for c in range(2):
-            for s in range(PASSES):
-                w2_raw[s, c] = load(w2, s, c * N // 2, N // 2, f"w2_raw{s}{c}")
-        nc.sync.dma_start(pos_t[0][:], pos1)
-        nc.sync.dma_start(pos_t[1][:], pos2)
-        gates = held([P, D, V], F32, "gates")
-        nc.sync.dma_start(out=gates[:], in_=gate[:, :P, :].rearrange("d p v -> p d v"))
+        for s, first, count in ((0, 0, 2), (1, 0, 2), (0, 2, 2), (1, 2, 1), (1, 3, 1)):
+            w2_raw[s, first] = load(w2, s, first * P, count * P, f"w2_raw{s}{first}")
+            if (s, first) == (0, 2):
+                nc.sync.dma_start(pos_t[0][:], pos1)
+            if (s, first) == (1, 2):
+                nc.sync.dma_start(pos_t[1][:], pos2)
 
         warm = keep.tile([P, 1], F32, name="warm")
         nc.vector.memset(warm[:], 0.0)
@@ -134,6 +141,17 @@ def tile_picked_sub_mlp_silu_sub_e_kernel(
             x_codes[s] = held([P, S], U32, f"x_codes{s}")
             x_scales[s] = held([P, S], U8, f"x_scales{s}")
             quantise(x_codes[s][:], x_scales[s][:], picked[:].rearrange("p n j -> p (n j)"))
+
+        spread = banks.tile([P, PACK, D, V // PACK], F32, name=f"bank{2 * BLOCKS - 1}")
+        for i in range(PACK):
+            column = gate_quads[:, i : i + 1].to_broadcast([P, P])
+            nc.tensor.transpose(spread[:, i].rearrange("p d q -> p (d q)"), column, identity[:])
+        gates = []
+        for d in range(D):
+            gates.append(held([P, V], F32, f"gates{d}"))
+            nc.scalar.activation(
+                gates[d][:].rearrange("p (q i) -> p q i", i=PACK), spread[:, :, d, :].rearrange("p i q -> p q i"), COPY
+            )
 
         idle = banks.tile([P, S], F32, name=f"bank{2 * BLOCKS - 1}")
         for i in range(WARM_PASSES):
@@ -202,77 +220,86 @@ def tile_picked_sub_mlp_silu_sub_e_kernel(
             h[1, nb] = held([P, P, PACK], BF16, f"h1{nb}")[:]
         last_pass_and_silu(1)
 
+        h_codes = [held([P, S], U32, f"h_codes{s}") for s in range(PASSES)]
         h_scales = [held([P, S], U8, f"h_scales{s}") for s in range(PASSES)]
-        h_codes_first = []
+        w2_grouped, w2_operand = {}, {}
+
+        def quantise_h(s, nodes, values):
+            quantise(h_codes[s][:, nodes], h_scales[s][:, nodes], values.rearrange("p n t -> p (n t)"))
+
+        def quantise_block(nb):
+            quantise_h(1, slice(nb * P, (nb + 1) * P), h[1, nb])
+
+        def cast_w2(s, first, count, on_scalar):
+            width = count * P
+            w2_grouped[s, first] = held([P, width, PACK], BF16, f"w2_grouped{s}{first}")
+            dst = w2_grouped[s, first][:].rearrange("p (c i) j -> p c j i", i=PACK)
+            src = w2_raw[s, first] if (s, first) in w2_raw else w2_raw[s, first - 1][:, :, P:]
+            cast(dst, src[:, :, :width].rearrange("p j (c i) -> p c j i", i=PACK), width // PACK if on_scalar else 0)
+
+        def quantise_w2(s, first, count):
+            codes = held([P, count * P], U32, f"w2_codes{s}{first}")
+            scales = held([P, count * P], U8, f"w2_scales{s}{first}")
+            quantise(codes[:], scales[:], w2_grouped[s, first][:].rearrange("p c j -> p (c j)"))
+            for i in range(count):
+                w2_operand[s, first + i] = codes[:, i * P : (i + 1) * P], scales[:, i * P : (i + 1) * P]
+
+        cast_w2(0, 0, 2, False)
         for half in range(2):
             nodes = slice(half * HALF, (half + 1) * HALF)
-            h_codes_first.append(held([P, HALF], U32, f"h_codes0{half}"))
-            quantise(h_codes_first[half][:], h_scales[0][:, nodes], h_first[:, nodes, :].rearrange("p n t -> p (n t)"))
+            quantise_h(0, nodes, h_first[:, nodes, :])
+        quantise_w2(0, 0, 2)
+        quantise_block(0)
+        cast_w2(1, 0, 2, False)
+        quantise_block(1)
+        quantise_w2(1, 0, 2)
+        quantise_block(2)
+        quantise_block(3)
 
-        w2_codes, w2_scales = {}, {}
+        total, y = {}, {}
 
-        def prepare_w2(first, count, on_scalar):
-            width = count * P
-            grouped = held([P, PASSES, width, PACK], BF16, f"w2_grouped{first}")
-            codes = held([P, PASSES, width], U32, f"w2_codes{first}")
-            scales = held([P, PASSES, width], U8, f"w2_scales{first}")
-            for s in range(PASSES):
-                dst = grouped[:, s].rearrange("p (c i) j -> p c j i", i=PACK)
-                src = w2_raw[s, first // 2][:, :, first % 2 * P : first % 2 * P + width]
-                cast(dst, src.rearrange("p j (c i) -> p c j i", i=PACK), width // PACK if on_scalar else 0)
-            quantise(
-                codes[:].rearrange("p s c -> p (s c)"),
-                scales[:].rearrange("p s c -> p (s c)"),
-                grouped[:].rearrange("p s c j -> p (s c j)"),
-            )
-            for i in range(count):
-                w2_codes[first + i] = codes[:, :, i * P : (i + 1) * P]
-                w2_scales[first + i] = scales[:, :, i * P : (i + 1) * P]
+        def pass2(result, mt, s, nodes):
+            multiply(result, w2_operand[s, mt], (h_codes[s][:, nodes], h_scales[s][:, nodes]), s == 0, s == 1)
 
-        prepare_w2(0, 2, False)
-        h_codes_second = held([P, S], U32, "h_codes1")
-        for nb in range(BLOCKS):
+        def copy_y(mt):
+            y[mt] = held([P, S], F32, f"y{mt}")
+            nc.scalar.activation(y[mt][:], total[mt][:], COPY)
+
+        everyone, last_block = slice(0, S), slice(S - P, S)
+        total[0] = banks.tile([P, S - P], F32, name="bank0")
+        total_last = banks.tile([P, P], F32, name=f"bank{2 * BLOCKS - 2}")
+        total[1] = banks.tile([P, S], F32, name="bank1")
+        pass2(total_last[:], 0, 0, last_block)
+        pass2(total[1][:], 1, 0, everyone)
+        for nb in range(BLOCKS - 1):
             nodes = slice(nb * P, (nb + 1) * P)
-            quantise(h_codes_second[:, nodes], h_scales[1][:, nodes], h[1, nb].rearrange("p n t -> p (n t)"))
+            for s in range(PASSES):
+                pass2(total[0][:, nodes], 0, s, nodes)
+        pass2(total_last[:], 0, 1, last_block)
+        pass2(total[1][:], 1, 1, everyone)
+        y[0] = held([P, S], F32, "y0")
+        nc.scalar.activation(y[0][:, : S - P], total[0][:], COPY)
+        nc.scalar.activation(y[0][:, last_block], total_last[:], COPY)
 
-        def h_operand(s, nodes):
-            if s == 1:
-                return h_codes_second[:, nodes], h_scales[1][:, nodes]
-            half = nodes.start // HALF
-            return h_codes_first[half][:, nodes.start - half * HALF : nodes.stop - half * HALF], h_scales[0][:, nodes]
-
-        y = {}
-
-        def product2(mt):
-            total = banks.tile([P, S], F32, name=f"bank{mt}")
-            y[mt] = held([P, S], F32, "w2_raw11" if mt == 2 else f"y{mt}")
-            if mt == 0:
-                steps = [(s, slice(nb * P, (nb + 1) * P), s == 0, s == 1) for nb in range(BLOCKS) for s in range(PASSES)]
-                copies = [slice(0, S - P), slice(S - P, S)]
-            else:
-                steps = [(0, slice(0, HALF), True, False), (0, slice(HALF, S), False, False), (1, slice(0, S), False, True)]
-                copies = [slice(0, S)]
-            for s, nodes, start, stop in steps:
-                multiply(total[:, nodes], (w2_codes[mt][:, s], w2_scales[mt][:, s]), h_operand(s, nodes), start, stop)
-            for nodes in copies:
-                nc.scalar.activation(y[mt][:, nodes], total[:, nodes], COPY)
-
-        product2(0)
-        prepare_w2(2, 1, False)
-        product2(1)
-        prepare_w2(3, 1, True)
-        product2(2)
-        product2(3)
+        for mt in (2, 3):
+            cast_w2(0, mt, 1, False)
+        for mt in (2, 3):
+            quantise_w2(0, mt, 1)
+            total[mt] = banks.tile([P, S], F32, name=f"bank{mt}")
+            pass2(total[mt][:], mt, 0, everyone)
+        cast_w2(1, 2, 1, True)
+        copy_y(1)
+        cast_w2(1, 3, 1, True)
 
         out_rows = out.rearrange("(m p) v -> p m v", p=P)
         terms = {}
 
         def fetch(mt, d):
             terms[mt, d] = held([P, V], F32, f"terms{mt}{d}")
-            nc.vector.tensor_tensor(terms[mt, d][:], y[mt][:].indirect(pos_t[d][:]), gates[:, d, :], MULT)
+            nc.vector.tensor_tensor(terms[mt, d][:], y[mt][:].indirect(pos_t[d][:]), gates[d][:], MULT)
 
         def add_by_transposes(mt):
-            turned = banks.tile([P, V], F32, name=f"bank{mt + 2}")
+            turned = banks.tile([P, V], F32, name=f"bank{7 if mt == 0 else 2}")
             for vb in range(V // P):
                 targets = slice(vb * P, (vb + 1) * P)
                 for d in range(D):
@@ -294,14 +321,22 @@ def tile_picked_sub_mlp_silu_sub_e_kernel(
             nc.scalar.activation(result[:], back[:], COPY)
             nc.scalar.dma_start(out=out_rows[:, mt, :], in_=result[:])
 
+        fetch(0, 0)
+        fetch(0, 1)
+        quantise_w2(1, 2, 1)
+        pass2(total[2][:], 2, 1, everyone)
+        fetch(1, 0)
+        fetch(1, 1)
+        quantise_w2(1, 3, 1)
+        pass2(total[3][:], 3, 1, everyone)
+        copy_y(2)
+        copy_y(3)
         for mt in range(TILES // 2):
+            add_by_transposes(mt)
+        for mt in range(TILES // 2, TILES):
             for d in range(D):
                 fetch(mt, d)
-            add_by_transposes(mt)
-        for d in range(D):
-            for mt in range(TILES // 2, TILES):
-                fetch(mt, d)
         for mt in range(TILES // 2, TILES):
-            result = keep.tile([P, V], F32, name=f"result{mt}")
+            result = held([P, V], F32, f"result{mt}")
             nc.vector.tensor_tensor(result[:], terms[mt, 0][:], terms[mt, 1][:], ADD)
             nc.sync.dma_start(out=out_rows[:, mt, :], in_=result[:])

@@ -36,11 +36,11 @@ TURNS = {
     "w2_grouped00": 1024,
     "h13": 4096,
     "w2_grouped02": 3584,
-    "w2_grouped03": 4608,
+    "w2_grouped12": 4608,
     "w2_raw02": 8192,
-    "w2_grouped12": 8192,
-    "w2_grouped13": 11264,
-    "w2_raw12": 16384,
+    "w2_grouped03": 8192,
+    "w2_grouped13": 9216,
+    "w2_raw03": 16384,
     "y1": 16384,
     "w2_raw13": 20480,
     "y2": 19456,
@@ -78,29 +78,24 @@ def tile_picked_sub_mlp_silu_sub_e_kernel(
             nc.sync.dma_start(out=raw[:], in_=pass_rows(matrix, s)[:, :, first : first + width])
             return raw[:]
 
+        gate_pairs = held([P, D, 2], F32, "gate_pairs")
+        nc.scalar.dma_start(out=gate_pairs[:], in_=gate[:, 0, :].rearrange("d (p i) -> p d i", i=2))
         for s in range(PASSES):
             for u in range(2):
                 x_raw[s, u] = held([P, 2, T], F32, f"x_raw{s}{u}")
                 nc.sync.dma_start(out=x_raw[s, u][:], in_=pass_rows(xT, s)[:, 2 * u : 2 * u + 2, :])
                 if (s, u) == (0, 0):
                     nc.sync.dma_start(offs_t[:], offs)
-                    gate_quads = held([P, PACK], F32, "gate_quads")
-                    for d in range(D):
-                        nc.sync.dma_start(
-                            out=gate_quads[d * V // PACK : (d + 1) * V // PACK, :],
-                            in_=gate[d, 0, :].rearrange("(q i) -> q i", i=PACK),
-                        )
         whole = load(w1, 0, 0, H, "w1_raw0")
         for b in range(2):
             w1_raw[b, 0] = [whole[:, :, b * PASS : (b + 1) * PASS]]
         w1_raw[0, 1] = [load(w1, 1, 0, PASS, "w1_raw01")]
         w1_raw[1, 1] = [load(w1, 1, PASS + c * PASS // 2, PASS // 2, f"w1_raw11{c}") for c in range(2)]
-        for s, first, count in ((0, 0, 2), (1, 0, 2), (0, 2, 2), (1, 2, 1), (1, 3, 1)):
+        for s, first, count in ((0, 0, 2), (1, 0, 2), (0, 2, 1), (1, 2, 1), (0, 3, 1), (1, 3, 1)):
             w2_raw[s, first] = load(w2, s, first * P, count * P, f"w2_raw{s}{first}")
-            if (s, first) == (0, 2):
-                nc.sync.dma_start(pos_t[0][:], pos1)
             if (s, first) == (1, 2):
-                nc.sync.dma_start(pos_t[1][:], pos2)
+                nc.sync.dma_start(pos_t[0][:], pos1)
+        nc.sync.dma_start(pos_t[1][:], pos2)
 
         warm = keep.tile([P, 1], F32, name="warm")
         nc.vector.memset(warm[:], 0.0)
@@ -142,15 +137,15 @@ def tile_picked_sub_mlp_silu_sub_e_kernel(
             x_scales[s] = held([P, S], U8, f"x_scales{s}")
             quantise(x_codes[s][:], x_scales[s][:], picked[:].rearrange("p n j -> p (n j)"))
 
-        spread = banks.tile([P, PACK, D, V // PACK], F32, name=f"bank{2 * BLOCKS - 1}")
-        for i in range(PACK):
-            column = gate_quads[:, i : i + 1].to_broadcast([P, P])
-            nc.tensor.transpose(spread[:, i].rearrange("p d q -> p (d q)"), column, identity[:])
+        spread = banks.tile([P, D, 2, P], F32, name=f"bank{2 * BLOCKS - 1}")
         gates = []
+        for d in range(D):
+            for i in range(2):
+                nc.tensor.transpose(spread[:, d, i], gate_pairs[:, d, i : i + 1].to_broadcast([P, P]), identity[:])
         for d in range(D):
             gates.append(held([P, V], F32, f"gates{d}"))
             nc.scalar.activation(
-                gates[d][:].rearrange("p (q i) -> p q i", i=PACK), spread[:, :, d, :].rearrange("p i q -> p q i"), COPY
+                gates[d][:].rearrange("p (q i) -> p q i", i=2), spread[:, d].rearrange("p i q -> p q i"), COPY
             )
 
         idle = banks.tile([P, S], F32, name=f"bank{2 * BLOCKS - 1}")
@@ -234,8 +229,7 @@ def tile_picked_sub_mlp_silu_sub_e_kernel(
             width = count * P
             w2_grouped[s, first] = held([P, width, PACK], BF16, f"w2_grouped{s}{first}")
             dst = w2_grouped[s, first][:].rearrange("p (c i) j -> p c j i", i=PACK)
-            src = w2_raw[s, first] if (s, first) in w2_raw else w2_raw[s, first - 1][:, :, P:]
-            cast(dst, src[:, :, :width].rearrange("p j (c i) -> p c j i", i=PACK), width // PACK if on_scalar else 0)
+            cast(dst, w2_raw[s, first].rearrange("p j (c i) -> p c j i", i=PACK), width // PACK if on_scalar else 0)
 
         def quantise_w2(s, first, count):
             codes = held([P, count * P], U32, f"w2_codes{s}{first}")
@@ -281,13 +275,17 @@ def tile_picked_sub_mlp_silu_sub_e_kernel(
         nc.scalar.activation(y[0][:, : S - P], total[0][:], COPY)
         nc.scalar.activation(y[0][:, last_block], total_last[:], COPY)
 
-        for mt in (2, 3):
-            cast_w2(0, mt, 1, False)
-        for mt in (2, 3):
-            quantise_w2(0, mt, 1)
-            total[mt] = banks.tile([P, S], F32, name=f"bank{mt}")
-            pass2(total[mt][:], mt, 0, everyone)
-        cast_w2(1, 2, 1, True)
+        def finish(mt, s):
+            quantise_w2(s, mt, 1)
+            if s == 0:
+                total[mt] = banks.tile([P, S], F32, name=f"bank{mt}")
+            pass2(total[mt][:], mt, s, everyone)
+
+        for s in range(PASSES):
+            cast_w2(s, 2, 1, False)
+        for s in range(PASSES):
+            finish(2, s)
+        cast_w2(0, 3, 1, True)
         copy_y(1)
         cast_w2(1, 3, 1, True)
 
@@ -323,12 +321,10 @@ def tile_picked_sub_mlp_silu_sub_e_kernel(
 
         fetch(0, 0)
         fetch(0, 1)
-        quantise_w2(1, 2, 1)
-        pass2(total[2][:], 2, 1, everyone)
+        finish(3, 0)
         fetch(1, 0)
         fetch(1, 1)
-        quantise_w2(1, 3, 1)
-        pass2(total[3][:], 3, 1, everyone)
+        finish(3, 1)
         copy_y(2)
         copy_y(3)
         for mt in range(TILES // 2):

@@ -25,7 +25,7 @@ BLOCKS = S // P
 TILES = N // P
 HALF = S // 2
 
-X_SCALAR = {(0, 0): 320, (0, 1): 320, (1, 0): 640, (1, 1): 576}
+X_SCALAR = {(0, 0): 320, (0, 1): 544, (1, 0): 864, (1, 1): 832}
 W1_SCALAR = {(0, 0): 44, (1, 0): 60, (0, 1): 42}
 W1_SHORT = 24
 WARM_PASSES = 4
@@ -34,10 +34,9 @@ TURNS = {
     "w1_grouped111": 0,
     "h_scales0": 0,
     "w2_grouped00": 1024,
-    "h13": 4096,
-    "w2_grouped02": 3584,
+    "h12": 4096,
     "w2_grouped12": 4608,
-    "w2_raw02": 8192,
+    "w2_raw12": 8192,
     "w2_grouped03": 8192,
     "w2_grouped13": 9216,
     "w2_raw03": 16384,
@@ -229,7 +228,7 @@ def tile_picked_sub_mlp_silu_sub_e_kernel(
             width = count * P
             w2_grouped[s, first] = held([P, width, PACK], BF16, f"w2_grouped{s}{first}")
             dst = w2_grouped[s, first][:].rearrange("p (c i) j -> p c j i", i=PACK)
-            cast(dst, w2_raw[s, first].rearrange("p j (c i) -> p c j i", i=PACK), width // PACK if on_scalar else 0)
+            cast(dst, w2_raw[s, first].rearrange("p j (c i) -> p c j i", i=PACK), on_scalar)
 
         def quantise_w2(s, first, count):
             codes = held([P, count * P], U32, f"w2_codes{s}{first}")
@@ -238,13 +237,13 @@ def tile_picked_sub_mlp_silu_sub_e_kernel(
             for i in range(count):
                 w2_operand[s, first + i] = codes[:, i * P : (i + 1) * P], scales[:, i * P : (i + 1) * P]
 
-        cast_w2(0, 0, 2, False)
+        cast_w2(0, 0, 2, 0)
         for half in range(2):
             nodes = slice(half * HALF, (half + 1) * HALF)
             quantise_h(0, nodes, h_first[:, nodes, :])
         quantise_w2(0, 0, 2)
         quantise_block(0)
-        cast_w2(1, 0, 2, False)
+        cast_w2(1, 0, 2, 0)
         quantise_block(1)
         quantise_w2(1, 0, 2)
         quantise_block(2)
@@ -282,12 +281,12 @@ def tile_picked_sub_mlp_silu_sub_e_kernel(
             pass2(total[mt][:], mt, s, everyone)
 
         for s in range(PASSES):
-            cast_w2(s, 2, 1, False)
+            cast_w2(s, 2, 1, 16 if s == 0 else 0)
         for s in range(PASSES):
             finish(2, s)
-        cast_w2(0, 3, 1, True)
+        cast_w2(0, 3, 1, P // PACK)
         copy_y(1)
-        cast_w2(1, 3, 1, True)
+        cast_w2(1, 3, 1, P // PACK)
 
         out_rows = out.rearrange("(m p) v -> p m v", p=P)
         terms = {}

@@ -28,6 +28,7 @@ HALF = S // 2
 X_SCALAR = {(0, 0): 320, (0, 1): 544, (1, 0): 864, (1, 1): 832}
 W1_SCALAR = {(0, 0): 44, (1, 0): 60, (0, 1): 42}
 W1_SHORT = 24
+BY_TILE_PAIRS = "p m j (u e) -> p u m j e"
 WARM_PASSES = 4
 
 TURNS = {
@@ -35,7 +36,9 @@ TURNS = {
     "h_scales0": 0,
     "w2_grouped00": 1024,
     "h12": 4096,
-    "w2_grouped12": 4608,
+    "w2_grouped02": 4096,
+    "h13": 5120,
+    "w2_grouped12": 5120,
     "w2_raw12": 8192,
     "w2_grouped03": 8192,
     "w2_grouped13": 9216,
@@ -106,11 +109,14 @@ def tile_picked_sub_mlp_silu_sub_e_kernel(
         def quantise(codes, scales, values):
             nc.vector.quantize_mx(out=codes.bitcast(FP8X4), scales=scales, in_=values)
 
-        def cast(dst, src, cut):
+        def cast(dst, src, cut, vector_order=None):
             if cut:
                 nc.scalar.activation(dst[:, :cut], src[:, :cut], COPY)
             if cut < src.shape[1]:
-                nc.vector.tensor_copy(dst[:, cut:], src[:, cut:])
+                rest = [dst[:, cut:], src[:, cut:]]
+                if vector_order:
+                    rest = [side.rearrange(vector_order, u=2) for side in rest]
+                nc.vector.tensor_copy(*rest)
 
         def multiply(result, stationary, moving, start, stop):
             nc.tensor.matmul_mx(
@@ -163,12 +169,12 @@ def tile_picked_sub_mlp_silu_sub_e_kernel(
                 src = raw.rearrange("p j (m t) -> p m j t", t=PACK)
                 if (b, s) == (1, 0):
                     rest = width - W1_SHORT
-                    nc.vector.tensor_copy(dst[:, rest:], src[:, rest:])
-                    cast(dst[:, :rest], src[:, :rest], W1_SCALAR[b, s])
+                    cast(dst[:, rest:], src[:, rest:], 0, BY_TILE_PAIRS)
+                    cast(dst[:, :rest], src[:, :rest], W1_SCALAR[b, s], BY_TILE_PAIRS)
                 elif (b, s) == (1, 1):
-                    cast(dst, src, width if c == 0 else 0)
+                    cast(dst, src, width if c == 0 else 0, BY_TILE_PAIRS)
                 else:
-                    cast(dst, src, W1_SCALAR[b, s])
+                    cast(dst, src, W1_SCALAR[b, s], BY_TILE_PAIRS)
                 columns = slice(c * width, (c + 1) * width)
                 for t in range(0, PACK, tiles_at_once):
                     some = slice(t, t + tiles_at_once)

@@ -49,7 +49,7 @@ TURNS = {
     "summed0": 21504,
     "gates0": 12288,
     "result2": 12288,
-    "w1_grouped010": 24576,
+    "w1_raw01": 24576,
     "w1_scales10": 24576,
 }
 
@@ -137,10 +137,17 @@ def tile_picked_sub_mlp_silu_sub_e_kernel(
                 pairs = held([P, T, 2], BF16, f"pairs{s}{u}")
                 cast(pairs, x_raw[s, u][:].rearrange("p e c -> p c e"), X_SCALAR[s, u])
                 window = pairs[:].rearrange("p c e -> p (c e)").bitcast(U32)
-                nc.vector.tensor_copy(words[:, :, u], window.indirect(offs_t[:]))
+                if (s, u) != (1, 1):
+                    nc.vector.tensor_copy(words[:, :, u], window.indirect(offs_t[:]))
             x_codes[s] = held([P, S], U32, f"x_codes{s}")
             x_scales[s] = held([P, S], U8, f"x_scales{s}")
-            quantise(x_codes[s][:], x_scales[s][:], picked[:].rearrange("p n j -> p (n j)"))
+            if s == 0:
+                quantise(x_codes[s][:], x_scales[s][:], picked[:].rearrange("p n j -> p (n j)"))
+        halves = [slice(half * HALF, (half + 1) * HALF) for half in range(2)]
+        for nodes in halves:
+            nc.vector.tensor_copy(words[:, nodes, 1], window.indirect(offs_t[:, nodes.start // 16 : nodes.stop // 16]))
+        for nodes in halves:
+            quantise(x_codes[1][:, nodes], x_scales[1][:, nodes], picked[:, nodes, :].rearrange("p n j -> p (n j)"))
 
         spread = banks.tile([P, D, 2, P], F32, name=f"bank{2 * BLOCKS - 1}")
         gates = []
@@ -155,7 +162,7 @@ def tile_picked_sub_mlp_silu_sub_e_kernel(
 
         idle = banks.tile([P, S], F32, name=f"bank{2 * BLOCKS - 1}")
         for i in range(WARM_PASSES):
-            multiply(idle[:], (x_codes[1][:, :P], x_scales[1][:, :P]), (x_codes[1][:], x_scales[1][:]), True, True)
+            multiply(idle[:], (x_codes[1][:, :P], x_scales[1][:, :P]), (x_codes[0][:], x_scales[0][:]), True, True)
 
         w1_codes, w1_scales = {}, {}
 

@@ -9,6 +9,7 @@ FLOPS = 2 * S * (K * H + H * N)
 F32 = mybir.dt.float32
 BF16 = mybir.dt.bfloat16
 U32 = mybir.dt.uint32
+I32 = mybir.dt.int32
 U16 = mybir.dt.uint16
 U8 = mybir.dt.uint8
 FP8X4 = mybir.dt.float8_e4m3fn_x4
@@ -25,7 +26,7 @@ BLOCKS = S // P
 TILES = N // P
 HALF = S // 2
 
-X_SCALAR = {(0, 0): 320, (0, 1): 544, (1, 0): 864, (1, 1): 832}
+X_SCALAR = {(0, 0): 384, (0, 1): 416, (1, 0): 720, (1, 1): 560}
 W1_SCALAR = {(0, 0): 44, (1, 0): 60, (0, 1): 42}
 W1_SHORT = 24
 BY_TILE_PAIRS = "p m j (u e) -> p u m j e"
@@ -130,24 +131,24 @@ def tile_picked_sub_mlp_silu_sub_e_kernel(
             )
 
         x_codes, x_scales = {}, {}
+        halves = [slice(half * HALF, (half + 1) * HALF) for half in range(2)]
         for s in range(PASSES):
             picked = held([P, S, PACK], BF16, f"picked{s}")
-            words = picked[:].rearrange("p n j -> p (n j)").bitcast(U32).rearrange("p (n u) -> p n u", u=2)
+            words = picked[:].rearrange("p n j -> p (n j)").bitcast(I32).rearrange("p (n u) -> p n u", u=2)
+            planes = held([P, 2, S], U32, f"planes{s}")
             for u in range(2):
                 pairs = held([P, T, 2], BF16, f"pairs{s}{u}")
                 cast(pairs, x_raw[s, u][:].rearrange("p e c -> p c e"), X_SCALAR[s, u])
                 window = pairs[:].rearrange("p c e -> p (c e)").bitcast(U32)
-                if (s, u) != (1, 1):
-                    nc.vector.tensor_copy(words[:, :, u], window.indirect(offs_t[:]))
+                for nodes in halves if u == 1 else [slice(0, S)]:
+                    entries = offs_t[:, nodes.start // 16 : nodes.stop // 16]
+                    nc.vector.tensor_copy(planes[:, u, nodes], window.indirect(entries))
+            for nodes in halves:
+                nc.vector.tensor_copy(words[:, nodes], planes[:].bitcast(I32)[:, :, nodes].rearrange("p u n -> p n u"))
             x_codes[s] = held([P, S], U32, f"x_codes{s}")
             x_scales[s] = held([P, S], U8, f"x_scales{s}")
-            if s == 0:
-                quantise(x_codes[s][:], x_scales[s][:], picked[:].rearrange("p n j -> p (n j)"))
-        halves = [slice(half * HALF, (half + 1) * HALF) for half in range(2)]
-        for nodes in halves:
-            nc.vector.tensor_copy(words[:, nodes, 1], window.indirect(offs_t[:, nodes.start // 16 : nodes.stop // 16]))
-        for nodes in halves:
-            quantise(x_codes[1][:, nodes], x_scales[1][:, nodes], picked[:, nodes, :].rearrange("p n j -> p (n j)"))
+            for nodes in halves:
+                quantise(x_codes[s][:, nodes], x_scales[s][:, nodes], picked[:, nodes, :].rearrange("p n j -> p (n j)"))
 
         spread = banks.tile([P, D, 2, P], F32, name=f"bank{2 * BLOCKS - 1}")
         gates = []

@@ -26,10 +26,10 @@ BLOCKS = S // P
 TILES = N // P
 HALF = S // 2
 
-X_SCALAR = {(0, 0): 384, (0, 1): 416, (1, 0): 720, (1, 1): 560}
-W1_SCALAR = {(0, 0): 44, (1, 0): 60, (0, 1): 42}
+X_SCALAR = {(0, 0): 384, (0, 1): 416, (1, 0): 880, (1, 1): 720}
+W1_SCALAR = {(0, 0): 52, (1, 0): 60, (0, 1): 42}
 W1_SHORT = 24
-BY_TILE_PAIRS = "p m j (u e) -> p u m j e"
+BY_TILE_PAIRS = "p m j (a e) -> p a m j e"
 WARM_PASSES = 4
 
 TURNS = {
@@ -116,7 +116,7 @@ def tile_picked_sub_mlp_silu_sub_e_kernel(
             if cut < src.shape[1]:
                 rest = [dst[:, cut:], src[:, cut:]]
                 if vector_order:
-                    rest = [side.rearrange(vector_order, u=2) for side in rest]
+                    rest = [side.rearrange(vector_order, a=2) for side in rest]
                 nc.vector.tensor_copy(*rest)
 
         def multiply(result, stationary, moving, start, stop):
@@ -238,11 +238,10 @@ def tile_picked_sub_mlp_silu_sub_e_kernel(
         def quantise_block(nb):
             quantise_h(1, slice(nb * P, (nb + 1) * P), h[1, nb])
 
-        def cast_w2(s, first, count, on_scalar):
-            width = count * P
-            w2_grouped[s, first] = held([P, width, PACK], BF16, f"w2_grouped{s}{first}")
+        def cast_w2(s, first, count, cut):
+            w2_grouped[s, first] = held([P, count * P, PACK], BF16, f"w2_grouped{s}{first}")
             dst = w2_grouped[s, first][:].rearrange("p (c i) j -> p c j i", i=PACK)
-            cast(dst, w2_raw[s, first].rearrange("p j (c i) -> p c j i", i=PACK), on_scalar)
+            cast(dst, w2_raw[s, first].rearrange("p j (c i) -> p c j i", i=PACK), cut)
 
         def quantise_w2(s, first, count):
             codes = held([P, count * P], U32, f"w2_codes{s}{first}")
@@ -252,8 +251,7 @@ def tile_picked_sub_mlp_silu_sub_e_kernel(
                 w2_operand[s, first + i] = codes[:, i * P : (i + 1) * P], scales[:, i * P : (i + 1) * P]
 
         cast_w2(0, 0, 2, 0)
-        for half in range(2):
-            nodes = slice(half * HALF, (half + 1) * HALF)
+        for nodes in halves:
             quantise_h(0, nodes, h_first[:, nodes, :])
         quantise_w2(0, 0, 2)
         quantise_block(0)
@@ -288,19 +286,20 @@ def tile_picked_sub_mlp_silu_sub_e_kernel(
         nc.scalar.activation(y[0][:, : S - P], total[0][:], COPY)
         nc.scalar.activation(y[0][:, last_block], total_last[:], COPY)
 
-        def finish(mt, s):
+        def quantise_and_multiply(mt, s):
             quantise_w2(s, mt, 1)
             if s == 0:
                 total[mt] = banks.tile([P, S], F32, name=f"bank{mt}")
             pass2(total[mt][:], mt, s, everyone)
 
+        quadruples = P // PACK
+        cast_w2(0, 2, 1, quadruples // 2)
+        cast_w2(1, 2, 1, 0)
         for s in range(PASSES):
-            cast_w2(s, 2, 1, 16 if s == 0 else 0)
-        for s in range(PASSES):
-            finish(2, s)
-        cast_w2(0, 3, 1, P // PACK)
+            quantise_and_multiply(2, s)
+        cast_w2(0, 3, 1, quadruples)
         copy_y(1)
-        cast_w2(1, 3, 1, P // PACK)
+        cast_w2(1, 3, 1, quadruples)
 
         out_rows = out.rearrange("(m p) v -> p m v", p=P)
         terms = {}
@@ -310,7 +309,7 @@ def tile_picked_sub_mlp_silu_sub_e_kernel(
             nc.vector.tensor_tensor(terms[mt, d][:], y[mt][:].indirect(pos_t[d][:]), gates[d][:], MULT)
 
         def add_by_transposes(mt):
-            turned = banks.tile([P, V], F32, name=f"bank{7 if mt == 0 else 2}")
+            turned = banks.tile([P, V], F32, name=f"bank{(2 * BLOCKS - 1, 2)[mt]}")
             for vb in range(V // P):
                 targets = slice(vb * P, (vb + 1) * P)
                 for d in range(D):
@@ -334,10 +333,10 @@ def tile_picked_sub_mlp_silu_sub_e_kernel(
 
         fetch(0, 0)
         fetch(0, 1)
-        finish(3, 0)
+        quantise_and_multiply(3, 0)
         fetch(1, 0)
         fetch(1, 1)
-        finish(3, 1)
+        quantise_and_multiply(3, 1)
         copy_y(2)
         copy_y(3)
         for mt in range(TILES // 2):

@@ -27,9 +27,9 @@ TILES = N // P
 HALF = S // 2
 
 X_SCALAR = {(0, 0): 384, (0, 1): 416, (1, 0): 880, (1, 1): 720}
-W1_SCALAR = {(0, 0): 52, (1, 0): 60, (0, 1): 42}
-W1_SHORT = 24
-BY_TILE_PAIRS = "p m j (a e) -> p a m j e"
+W1_SCALAR = {(0, 0): 26, (1, 0): 30, (0, 1): 22}
+W1_SHORT = 12
+RUN = 8
 WARM_PASSES = 4
 
 TURNS = {
@@ -110,14 +110,11 @@ def tile_picked_sub_mlp_silu_sub_e_kernel(
         def quantise(codes, scales, values):
             nc.vector.quantize_mx(out=codes.bitcast(FP8X4), scales=scales, in_=values)
 
-        def cast(dst, src, cut, vector_order=None):
+        def cast(dst, src, cut):
             if cut:
-                nc.scalar.activation(dst[:, :cut], src[:, :cut], COPY)
+                nc.scalar.copy(dst[:, :cut], src[:, :cut])
             if cut < src.shape[1]:
-                rest = [dst[:, cut:], src[:, cut:]]
-                if vector_order:
-                    rest = [side.rearrange(vector_order, a=2) for side in rest]
-                nc.vector.tensor_copy(*rest)
+                nc.vector.tensor_copy(dst[:, cut:], src[:, cut:])
 
         def multiply(result, stationary, moving, start, stop):
             nc.tensor.matmul_mx(
@@ -173,16 +170,17 @@ def tile_picked_sub_mlp_silu_sub_e_kernel(
             width = P // len(w1_raw[b, s])
             for c, raw in enumerate(w1_raw[b, s]):
                 grouped = held([P, PACK, width, PACK], BF16, f"w1_grouped{b}{s}{c}")
-                dst = grouped[:].rearrange("p t m j -> p m j t")
-                src = raw.rearrange("p j (m t) -> p m j t", t=PACK)
+                dst = grouped[:].rearrange("p t (m n) j -> p m j n t", n=RUN // PACK)
+                src = raw.rearrange("p j (m n t) -> p m j n t", n=RUN // PACK, t=PACK)
+                runs = src.shape[1]
                 if (b, s) == (1, 0):
-                    rest = width - W1_SHORT
-                    cast(dst[:, rest:], src[:, rest:], 0, BY_TILE_PAIRS)
-                    cast(dst[:, :rest], src[:, :rest], W1_SCALAR[b, s], BY_TILE_PAIRS)
+                    rest = runs - W1_SHORT
+                    cast(dst[:, rest:], src[:, rest:], 0)
+                    cast(dst[:, :rest], src[:, :rest], W1_SCALAR[b, s])
                 elif (b, s) == (1, 1):
-                    cast(dst, src, width if c == 0 else 0, BY_TILE_PAIRS)
+                    cast(dst, src, runs if c == 0 else 0)
                 else:
-                    cast(dst, src, W1_SCALAR[b, s], BY_TILE_PAIRS)
+                    cast(dst, src, W1_SCALAR[b, s])
                 columns = slice(c * width, (c + 1) * width)
                 for t in range(0, PACK, tiles_at_once):
                     some = slice(t, t + tiles_at_once)
@@ -240,8 +238,8 @@ def tile_picked_sub_mlp_silu_sub_e_kernel(
 
         def cast_w2(s, first, count, cut):
             w2_grouped[s, first] = held([P, count * P, PACK], BF16, f"w2_grouped{s}{first}")
-            dst = w2_grouped[s, first][:].rearrange("p (c i) j -> p c j i", i=PACK)
-            cast(dst, w2_raw[s, first].rearrange("p j (c i) -> p c j i", i=PACK), cut)
+            dst = w2_grouped[s, first][:].rearrange("p (c i) j -> p c j i", i=RUN)
+            cast(dst, w2_raw[s, first].rearrange("p j (c i) -> p c j i", i=RUN), cut)
 
         def quantise_w2(s, first, count):
             codes = held([P, count * P], U32, f"w2_codes{s}{first}")
@@ -292,14 +290,14 @@ def tile_picked_sub_mlp_silu_sub_e_kernel(
                 total[mt] = banks.tile([P, S], F32, name=f"bank{mt}")
             pass2(total[mt][:], mt, s, everyone)
 
-        quadruples = P // PACK
-        cast_w2(0, 2, 1, quadruples // 2)
+        runs = P // RUN
+        cast_w2(0, 2, 1, runs // 2)
         cast_w2(1, 2, 1, 0)
         for s in range(PASSES):
             quantise_and_multiply(2, s)
-        cast_w2(0, 3, 1, quadruples)
+        cast_w2(0, 3, 1, runs)
         copy_y(1)
-        cast_w2(1, 3, 1, quadruples)
+        cast_w2(1, 3, 1, runs)
 
         out_rows = out.rearrange("(m p) v -> p m v", p=P)
         terms = {}

@@ -33,9 +33,10 @@ RUN = 8
 WARM_PASSES = 4
 
 TURNS = {
-    "w1_grouped111": 0,
+    "w1_raw111": 0,
     "h_scales0": 0,
-    "w2_grouped00": 1024,
+    "h_first0": 32768,
+    "w2_grouped00": 32768,
     "h12": 4096,
     "w2_grouped02": 4096,
     "h13": 5120,
@@ -215,9 +216,9 @@ def tile_picked_sub_mlp_silu_sub_e_kernel(
             product1(0, 0, nb)
         prepare_w1(0, 1, 2)
         prepare_w1(1, 0, PACK)
-        h_first = held([P, S, PACK], BF16, "w1_raw110")
+        h_first = [held([P, HALF, PACK], BF16, f"h_first{half}") for half in range(2)]
         for nb in range(BLOCKS):
-            h[0, nb] = h_first[:, nb * P : (nb + 1) * P, :]
+            h[0, nb] = h_first[nb // 2][:, nb % 2 * P : (nb % 2 + 1) * P, :]
         last_pass_and_silu(0)
         for nb in range(BLOCKS):
             product1(1, 0, nb)
@@ -248,9 +249,9 @@ def tile_picked_sub_mlp_silu_sub_e_kernel(
             for i in range(count):
                 w2_operand[s, first + i] = codes[:, i * P : (i + 1) * P], scales[:, i * P : (i + 1) * P]
 
+        quantise_h(0, halves[0], h_first[0][:])
         cast_w2(0, 0, 2, 0)
-        for nodes in halves:
-            quantise_h(0, nodes, h_first[:, nodes, :])
+        quantise_h(0, halves[1], h_first[1][:])
         quantise_w2(0, 0, 2)
         quantise_block(0)
         cast_w2(1, 0, 2, 0)
@@ -258,31 +259,32 @@ def tile_picked_sub_mlp_silu_sub_e_kernel(
         quantise_w2(1, 0, 2)
         quantise_block(2)
         quantise_block(3)
+        runs = P // RUN
+        cast_w2(0, 2, 1, runs // 2)
 
         total, y = {}, {}
 
-        def pass2(result, mt, s, nodes):
-            multiply(result, w2_operand[s, mt], (h_codes[s][:, nodes], h_scales[s][:, nodes]), s == 0, s == 1)
+        def pass2(result, mt, s, nodes, last=True):
+            moving = h_codes[s][:, nodes], h_scales[s][:, nodes]
+            multiply(result, w2_operand[s, mt], moving, s == 0, s == 1 and last)
 
         def copy_y(mt):
             y[mt] = held([P, S], F32, f"y{mt}")
             nc.scalar.activation(y[mt][:], total[mt][:], COPY)
 
-        everyone, last_block = slice(0, S), slice(S - P, S)
-        total[0] = banks.tile([P, S - P], F32, name="bank0")
-        total_last = banks.tile([P, P], F32, name=f"bank{2 * BLOCKS - 2}")
+        everyone = slice(0, S)
+        total[0] = [banks.tile([P, HALF], F32, name=f"bank{bank}") for bank in (0, 2 * BLOCKS - 2)]
         total[1] = banks.tile([P, S], F32, name="bank1")
-        pass2(total_last[:], 0, 0, last_block)
+        for half, nodes in enumerate(halves):
+            pass2(total[0][half][:], 0, 0, nodes, last=False)
         pass2(total[1][:], 1, 0, everyone)
-        for nb in range(BLOCKS - 1):
+        for nb in range(BLOCKS):
             nodes = slice(nb * P, (nb + 1) * P)
-            for s in range(PASSES):
-                pass2(total[0][:, nodes], 0, s, nodes)
-        pass2(total_last[:], 0, 1, last_block)
+            pass2(total[0][nb // 2][:, nb % 2 * P : (nb % 2 + 1) * P], 0, 1, nodes, last=nb % 2 == 1)
         pass2(total[1][:], 1, 1, everyone)
         y[0] = held([P, S], F32, "y0")
-        nc.scalar.activation(y[0][:, : S - P], total[0][:], COPY)
-        nc.scalar.activation(y[0][:, last_block], total_last[:], COPY)
+        for half, nodes in enumerate(halves):
+            nc.scalar.activation(y[0][:, nodes], total[0][half][:], COPY)
 
         def quantise_and_multiply(mt, s):
             quantise_w2(s, mt, 1)
@@ -290,8 +292,6 @@ def tile_picked_sub_mlp_silu_sub_e_kernel(
                 total[mt] = banks.tile([P, S], F32, name=f"bank{mt}")
             pass2(total[mt][:], mt, s, everyone)
 
-        runs = P // RUN
-        cast_w2(0, 2, 1, runs // 2)
         cast_w2(1, 2, 1, 0)
         for s in range(PASSES):
             quantise_and_multiply(2, s)

@@ -45,10 +45,11 @@ TURNS = {
     "w2_grouped03": 8192,
     "w2_grouped13": 9216,
     "w2_raw03": 16384,
-    "y1": 16384,
+    "terms10": 16384,
     "w2_raw13": 20480,
-    "y2": 19456,
-    "summed0": 21504,
+    "y2": 18688,
+    "terms11": 20736,
+    "summed0": 21760,
     "gates0": 12288,
     "result2": 12288,
     "w1_raw01": 24576,
@@ -321,7 +322,7 @@ def tile_picked_sub_mlp_silu_sub_e_kernel(
                     )
             summed = held([P, V], F32, f"summed{mt}")
             nc.scalar.activation(summed[:], turned[:], COPY)
-            back = banks.tile([P, V], F32, name=f"bank{BLOCKS + mt}")
+            back = banks.tile([P, V], F32, name=f"bank{(3, BLOCKS + 1)[mt]}")
             for vb in range(V // P):
                 part = slice(vb * P, (vb + 1) * P)
                 nc.tensor.transpose(back[:, part], summed[:, part], identity[:])
@@ -333,8 +334,8 @@ def tile_picked_sub_mlp_silu_sub_e_kernel(
         fetch(0, 1)
         quantise_and_multiply(3, 0)
         fetch(1, 0)
-        fetch(1, 1)
         quantise_and_multiply(3, 1)
+        fetch(1, 1)
         copy_y(2)
         copy_y(3)
         for mt in range(TILES // 2):

@@ -27,10 +27,10 @@ TILES = N // P
 HALF = S // 2
 
 X_SCALAR = {(0, 0): 384, (0, 1): 416, (1, 0): 880, (1, 1): 720}
-W1_SCALAR = {(0, 0): 26, (1, 0): 30, (0, 1): 22}
-W1_SHORT = 12
-RUN = 8
-WARM_PASSES = 4
+W1_SCALAR = {(0, 0): 52, (1, 0): 60, (0, 1): 44}
+W1_SHORT = 24
+RUN = 4
+WARM_PASSES = 2
 
 TURNS = {
     "w1_raw111": 0,
@@ -162,7 +162,7 @@ def tile_picked_sub_mlp_silu_sub_e_kernel(
 
         idle = banks.tile([P, S], F32, name=f"bank{2 * BLOCKS - 1}")
         for i in range(WARM_PASSES):
-            multiply(idle[:], (x_codes[1][:, :P], x_scales[1][:, :P]), (x_codes[0][:], x_scales[0][:]), True, True)
+            multiply(idle[:], (x_codes[1][:, S - P :], x_scales[1][:, S - P :]), (x_codes[0][:], x_scales[0][:]), True, True)
 
         w1_codes, w1_scales = {}, {}
 
@@ -172,8 +172,8 @@ def tile_picked_sub_mlp_silu_sub_e_kernel(
             width = P // len(w1_raw[b, s])
             for c, raw in enumerate(w1_raw[b, s]):
                 grouped = held([P, PACK, width, PACK], BF16, f"w1_grouped{b}{s}{c}")
-                dst = grouped[:].rearrange("p t (m n) j -> p m j n t", n=RUN // PACK)
-                src = raw.rearrange("p j (m n t) -> p m j n t", n=RUN // PACK, t=PACK)
+                dst = grouped[:].rearrange("p t m (a e) -> p m a t e", e=2)
+                src = raw.rearrange("p (a e) (m t) -> p m a t e", e=2, t=RUN)
                 runs = src.shape[1]
                 if (b, s) == (1, 0):
                     rest = runs - W1_SHORT
@@ -240,8 +240,8 @@ def tile_picked_sub_mlp_silu_sub_e_kernel(
 
         def cast_w2(s, first, count, cut):
             w2_grouped[s, first] = held([P, count * P, PACK], BF16, f"w2_grouped{s}{first}")
-            dst = w2_grouped[s, first][:].rearrange("p (c i) j -> p c j i", i=RUN)
-            cast(dst, w2_raw[s, first].rearrange("p j (c i) -> p c j i", i=RUN), cut)
+            dst = w2_grouped[s, first][:].rearrange("p (c i) (a e) -> p c a i e", i=RUN, e=2)
+            cast(dst, w2_raw[s, first].rearrange("p (a e) (c i) -> p c a i e", i=RUN, e=2), cut)
 
         def quantise_w2(s, first, count):
             codes = held([P, count * P], U32, f"w2_codes{s}{first}")

@@ -40,12 +40,12 @@ TURNS = {
     "h12": 4096,
     "w2_grouped02": 4096,
     "h13": 5120,
-    "w2_grouped12": 5120,
-    "w2_raw12": 8192,
-    "w2_grouped03": 8192,
+    "w2_grouped03": 5120,
+    "w2_raw02": 8192,
+    "w2_grouped12": 8192,
     "w2_grouped13": 9216,
-    "w2_raw03": 16384,
-    "terms10": 16384,
+    "w2_raw12": 16384,
+    "terms01": 16384,
     "w2_raw13": 20480,
     "y2": 18688,
     "terms11": 20736,
@@ -96,11 +96,12 @@ def tile_picked_sub_mlp_silu_sub_e_kernel(
             w1_raw[b, 0] = [whole[:, :, b * PASS : (b + 1) * PASS]]
         w1_raw[0, 1] = [load(w1, 1, 0, PASS, "w1_raw01")]
         w1_raw[1, 1] = [load(w1, 1, PASS + c * PASS // 2, PASS // 2, f"w1_raw11{c}") for c in range(2)]
-        for s, first, count in ((0, 0, 2), (1, 0, 2), (0, 2, 1), (1, 2, 1), (0, 3, 1), (1, 3, 1)):
+        for s, first, count in ((0, 0, 2), (1, 0, 2), (0, 2, 2), (1, 2, 1), (1, 3, 1)):
             w2_raw[s, first] = load(w2, s, first * P, count * P, f"w2_raw{s}{first}")
             if (s, first) == (1, 2):
                 nc.sync.dma_start(pos_t[0][:], pos1)
-        nc.sync.dma_start(pos_t[1][:], pos2)
+                nc.sync.dma_start(pos_t[1][:], pos2)
+        w2_raw[0, 2], w2_raw[0, 3] = w2_raw[0, 2][:, :, :P], w2_raw[0, 2][:, :, P:]
 
         warm = keep.tile([P, 1], F32, name="warm")
         nc.vector.memset(warm[:], 0.0)
@@ -293,10 +294,10 @@ def tile_picked_sub_mlp_silu_sub_e_kernel(
                 total[mt] = banks.tile([P, S], F32, name=f"bank{mt}")
             pass2(total[mt][:], mt, s, everyone)
 
-        cast_w2(1, 2, 1, 0)
-        for s in range(PASSES):
-            quantise_and_multiply(2, s)
-        cast_w2(0, 3, 1, runs)
+        cast_w2(0, 3, 1, 0)
+        for mt in (2, 3):
+            quantise_and_multiply(mt, 0)
+        cast_w2(1, 2, 1, runs)
         copy_y(1)
         cast_w2(1, 3, 1, runs)
 
@@ -331,8 +332,8 @@ def tile_picked_sub_mlp_silu_sub_e_kernel(
             nc.scalar.dma_start(out=out_rows[:, mt, :], in_=result[:])
 
         fetch(0, 0)
+        quantise_and_multiply(2, 1)
         fetch(0, 1)
-        quantise_and_multiply(3, 0)
         fetch(1, 0)
         quantise_and_multiply(3, 1)
         fetch(1, 1)
@@ -340,10 +341,20 @@ def tile_picked_sub_mlp_silu_sub_e_kernel(
         copy_y(3)
         for mt in range(TILES // 2):
             add_by_transposes(mt)
-        for mt in range(TILES // 2, TILES):
-            for d in range(D):
-                fetch(mt, d)
-        for mt in range(TILES // 2, TILES):
-            result = held([P, V], F32, f"result{mt}")
-            nc.vector.tensor_tensor(result[:], terms[mt, 0][:], terms[mt, 1][:], ADD)
-            nc.sync.dma_start(out=out_rows[:, mt, :], in_=result[:])
+        def add_and_store(mt, targets, name):
+            result = held([P, targets.stop - targets.start], F32, name)
+            nc.vector.tensor_tensor(result[:], terms[mt, 0][:, targets], terms[mt, 1][:, targets], ADD)
+            nc.sync.dma_start(out=out_rows[:, mt, targets], in_=result[:])
+
+        parts = [slice(0, P), slice(P, V)]
+        fetch(2, 0)
+        fetch(2, 1)
+        fetch(3, 0)
+        terms[3, 1] = held([P, V], F32, "terms31")
+        for i, targets in enumerate(parts):
+            entries = pos_t[1][:, targets.start // 16 : targets.stop // 16]
+            nc.vector.tensor_tensor(terms[3, 1][:, targets], y[3][:].indirect(entries), gates[1][:, targets], MULT)
+            if i == 0:
+                add_and_store(2, slice(0, V), "result2")
+        for i, targets in enumerate(parts):
+            add_and_store(3, targets, f"result3{i}")

@@ -54,6 +54,8 @@ TURNS = {
     "result2": 12288,
     "w1_raw01": 24576,
     "w1_scales10": 24576,
+    "x_raw11": 36864,
+    "gate_columns": 36864,
 }
 
 
@@ -83,8 +85,9 @@ def tile_picked_sub_mlp_silu_sub_e_kernel(
             nc.sync.dma_start(out=raw[:], in_=pass_rows(matrix, s)[:, :, first : first + width])
             return raw[:]
 
-        gate_pairs = held([P, D, 2], F32, "gate_pairs")
-        nc.scalar.dma_start(out=gate_pairs[:], in_=gate[:, 0, :].rearrange("d (p i) -> p d i", i=2))
+        gate_rows = held([P, V], F32, "gate_rows")
+        nc.vector.memset(gate_rows[:], 0.0)
+        nc.scalar.dma_start(out=gate_rows[:D, :], in_=gate[:, 0, :])
         for s in range(PASSES):
             for u in range(2):
                 x_raw[s, u] = held([P, 2, T], F32, f"x_raw{s}{u}")
@@ -150,16 +153,19 @@ def tile_picked_sub_mlp_silu_sub_e_kernel(
             for nodes in halves:
                 quantise(x_codes[s][:, nodes], x_scales[s][:, nodes], picked[:, nodes, :].rearrange("p n j -> p (n j)"))
 
-        spread = banks.tile([P, D, 2, P], F32, name=f"bank{2 * BLOCKS - 1}")
+        upright = banks.tile([P, V // P, P], F32, name=f"bank{2 * BLOCKS - 2}")
+        for vb in range(V // P):
+            nc.tensor.transpose(upright[:, vb], gate_rows[:, vb * P : (vb + 1) * P], identity[:])
+        gate_columns = held([P, V // P, D], F32, "gate_columns")
+        nc.scalar.activation(gate_columns[:], upright[:, :, :D], COPY)
+        spread = banks.tile([P, D, V // P, P], F32, name=f"bank{2 * BLOCKS - 1}")
         gates = []
         for d in range(D):
-            for i in range(2):
-                nc.tensor.transpose(spread[:, d, i], gate_pairs[:, d, i : i + 1].to_broadcast([P, P]), identity[:])
+            for vb in range(V // P):
+                nc.tensor.transpose(spread[:, d, vb], gate_columns[:, vb, d : d + 1].to_broadcast([P, P]), identity[:])
         for d in range(D):
             gates.append(held([P, V], F32, f"gates{d}"))
-            nc.scalar.activation(
-                gates[d][:].rearrange("p (q i) -> p q i", i=2), spread[:, d].rearrange("p i q -> p q i"), COPY
-            )
+            nc.scalar.activation(gates[d][:], spread[:, d].rearrange("p b q -> p (b q)"), COPY)
 
         idle = banks.tile([P, S], F32, name=f"bank{2 * BLOCKS - 1}")
         for i in range(WARM_PASSES):

@@ -35,13 +35,13 @@ WARM_PASSES = 2
 TURNS = {
     "w1_raw111": 0,
     "h_scales0": 0,
+    "w2_grouped00": 1024,
     "h_first0": 32768,
-    "w2_grouped00": 32768,
-    "h12": 4096,
-    "w2_grouped02": 4096,
+    "w2_grouped10": 32768,
+    "w2_grouped02": 32768,
     "h13": 5120,
     "w2_grouped03": 5120,
-    "w2_raw02": 8192,
+    "w2_codes10": 9216 - 512,
     "w2_grouped12": 8192,
     "w2_grouped13": 9216,
     "w2_raw12": 16384,
@@ -54,8 +54,6 @@ TURNS = {
     "result2": 12288,
     "w1_raw01": 24576,
     "w1_scales10": 24576,
-    "x_raw11": 36864,
-    "gate_columns": 36864,
 }
 
 
@@ -85,9 +83,8 @@ def tile_picked_sub_mlp_silu_sub_e_kernel(
             nc.sync.dma_start(out=raw[:], in_=pass_rows(matrix, s)[:, :, first : first + width])
             return raw[:]
 
-        gate_rows = held([P, V], F32, "gate_rows")
-        nc.vector.memset(gate_rows[:], 0.0)
-        nc.scalar.dma_start(out=gate_rows[:D, :], in_=gate[:, 0, :])
+        gate_pairs = held([P, D, 2], F32, "gate_pairs")
+        nc.scalar.dma_start(out=gate_pairs[:], in_=gate[:, 0, :].rearrange("d (p i) -> p d i", i=2))
         for s in range(PASSES):
             for u in range(2):
                 x_raw[s, u] = held([P, 2, T], F32, f"x_raw{s}{u}")
@@ -153,19 +150,16 @@ def tile_picked_sub_mlp_silu_sub_e_kernel(
             for nodes in halves:
                 quantise(x_codes[s][:, nodes], x_scales[s][:, nodes], picked[:, nodes, :].rearrange("p n j -> p (n j)"))
 
-        upright = banks.tile([P, V // P, P], F32, name=f"bank{2 * BLOCKS - 2}")
-        for vb in range(V // P):
-            nc.tensor.transpose(upright[:, vb], gate_rows[:, vb * P : (vb + 1) * P], identity[:])
-        gate_columns = held([P, V // P, D], F32, "gate_columns")
-        nc.scalar.activation(gate_columns[:], upright[:, :, :D], COPY)
-        spread = banks.tile([P, D, V // P, P], F32, name=f"bank{2 * BLOCKS - 1}")
+        spread = banks.tile([P, D, 2, P], F32, name=f"bank{2 * BLOCKS - 1}")
         gates = []
         for d in range(D):
-            for vb in range(V // P):
-                nc.tensor.transpose(spread[:, d, vb], gate_columns[:, vb, d : d + 1].to_broadcast([P, P]), identity[:])
+            for i in range(2):
+                nc.tensor.transpose(spread[:, d, i], gate_pairs[:, d, i : i + 1].to_broadcast([P, P]), identity[:])
         for d in range(D):
             gates.append(held([P, V], F32, f"gates{d}"))
-            nc.scalar.activation(gates[d][:], spread[:, d].rearrange("p b q -> p (b q)"), COPY)
+            nc.scalar.activation(
+                gates[d][:].rearrange("p (q i) -> p q i", i=2), spread[:, d].rearrange("p i q -> p q i"), COPY
+            )
 
         idle = banks.tile([P, S], F32, name=f"bank{2 * BLOCKS - 1}")
         for i in range(WARM_PASSES):
@@ -257,16 +251,14 @@ def tile_picked_sub_mlp_silu_sub_e_kernel(
             for i in range(count):
                 w2_operand[s, first + i] = codes[:, i * P : (i + 1) * P], scales[:, i * P : (i + 1) * P]
 
-        quantise_h(0, halves[0], h_first[0][:])
         cast_w2(0, 0, 2, 0)
-        quantise_h(0, halves[1], h_first[1][:])
+        quantise_h(0, halves[0], h_first[0][:])
         quantise_w2(0, 0, 2)
-        quantise_block(0)
         cast_w2(1, 0, 2, 0)
-        quantise_block(1)
+        quantise_h(0, halves[1], h_first[1][:])
         quantise_w2(1, 0, 2)
-        quantise_block(2)
-        quantise_block(3)
+        for nb in range(BLOCKS):
+            quantise_block(nb)
         runs = P // RUN
         cast_w2(0, 2, 1, runs // 2)
 

from contextlib import ExitStack

import concourse.mybir as mybir
from concourse.masks import make_identity

K, T, S, H, N, V, D = 1024, 1024, 512, 1024, 512, 256, 2
FLOPS = 2 * S * (K * H + H * N)

F32 = mybir.dt.float32
BF16 = mybir.dt.bfloat16
U32 = mybir.dt.uint32
I32 = mybir.dt.int32
U16 = mybir.dt.uint16
U8 = mybir.dt.uint8
FP8X4 = mybir.dt.float8_e4m3fn_x4
COPY = mybir.ActivationFunctionType.Copy
SILU = mybir.ActivationFunctionType.Silu
MULT = mybir.AluOpType.mult
ADD = mybir.AluOpType.add

P = 128
PACK = 4
PASS = P * PACK
PASSES = K // PASS
BLOCKS = S // P
TILES = N // P
HALF = S // 2

X_SCALAR = {(0, 0): 384, (0, 1): 416, (1, 0): 880, (1, 1): 720}
W1_SCALAR = {(0, 0): 52, (1, 0): 60, (0, 1): 44}
W1_SHORT = 24
RUN = 4
WARM_PASSES = 2

TURNS = {
    "w1_raw111": 0,
    "h_scales0": 0,
    "w2_grouped00": 1024,
    "h_first0": 32768,
    "w2_grouped10": 32768,
    "w2_grouped02": 32768,
    "h13": 5120,
    "w2_grouped03": 5120,
    "w2_codes10": 9216 - 512,
    "w2_grouped12": 8192,
    "w2_grouped13": 9216,
    "w2_raw12": 16384,
    "terms01": 16384,
    "w2_raw13": 20480,
    "y2": 18688,
    "terms11": 20736,
    "summed0": 21760,
    "gates0": 12288,
    "result2": 12288,
    "w1_raw01": 24576,
    "w1_scales10": 24576,
}


def tile_picked_sub_mlp_silu_sub_e_kernel(
    tc, xT, w1, w2, gate, offs, pos1, pos2, out
):
    nc = tc.nc
    with ExitStack() as ctx:
        keep = ctx.enter_context(tc.tile_pool(name="keep", bufs=1))
        banks = ctx.enter_context(tc.psum_pool(name="banks", bufs=1))
        turns = ctx.enter_context(tc.tile_pool(name="turns", bufs=1))

        def held(shape, dtype, name):
            if name in TURNS:
                return turns.tile(shape, dtype, name=name, align_bytes=64, offset=TURNS[name])
            return keep.tile(shape, dtype, name=name, align_bytes=64)

        def pass_rows(matrix, s):
            return matrix[s * PASS : (s + 1) * PASS, :].rearrange("(p j) c -> p j c", j=PACK)

        offs_t = keep.tile([P, S // 16], U16, name="offs_t")
        pos_t = [keep.tile([P, V // 16], U16, name=f"pos_t{d}") for d in range(D)]
        x_raw, w1_raw, w2_raw = {}, {}, {}

        def load(matrix, s, first, width, name):
            raw = held([P, PACK, width], F32, name)
            nc.sync.dma_start(out=raw[:], in_=pass_rows(matrix, s)[:, :, first : first + width])
            return raw[:]

        gate_pairs = held([P, D, 2], F32, "gate_pairs")
        nc.scalar.dma_start(out=gate_pairs[:], in_=gate[:, 0, :].rearrange("d (p i) -> p d i", i=2))
        for s in range(PASSES):
            for u in range(2):
                x_raw[s, u] = held([P, 2, T], F32, f"x_raw{s}{u}")
                nc.sync.dma_start(out=x_raw[s, u][:], in_=pass_rows(xT, s)[:, 2 * u : 2 * u + 2, :])
                if (s, u) == (0, 0):
                    nc.sync.dma_start(offs_t[:], offs)
        whole = load(w1, 0, 0, H, "w1_raw0")
        for b in range(2):
            w1_raw[b, 0] = [whole[:, :, b * PASS : (b + 1) * PASS]]
        w1_raw[0, 1] = [load(w1, 1, 0, PASS, "w1_raw01")]
        w1_raw[1, 1] = [load(w1, 1, PASS + c * PASS // 2, PASS // 2, f"w1_raw11{c}") for c in range(2)]
        for s, first, count in ((0, 0, 2), (1, 0, 2), (0, 2, 2), (1, 2, 1), (1, 3, 1)):
            w2_raw[s, first] = load(w2, s, first * P, count * P, f"w2_raw{s}{first}")
            if (s, first) == (1, 2):
                nc.sync.dma_start(pos_t[0][:], pos1)
                nc.sync.dma_start(pos_t[1][:], pos2)
        w2_raw[0, 2], w2_raw[0, 3] = w2_raw[0, 2][:, :, :P], w2_raw[0, 2][:, :, P:]

        warm = keep.tile([P, 1], F32, name="warm")
        nc.vector.memset(warm[:], 0.0)
        nc.scalar.activation(warm[:], warm[:], SILU)

        identity = held([P, P], F32, "identity")
        make_identity(nc, identity[:])

        def quantise(codes, scales, values):
            nc.vector.quantize_mx(out=codes.bitcast(FP8X4), scales=scales, in_=values)

        def cast(dst, src, cut):
            if cut:
                nc.scalar.copy(dst[:, :cut], src[:, :cut])
            if cut < src.shape[1]:
                nc.vector.tensor_copy(dst[:, cut:], src[:, cut:])

        def multiply(result, stationary, moving, start, stop):
            nc.tensor.matmul_mx(
                out=result,
                lhsT=stationary[0].bitcast(FP8X4),
                lhsT_scale=stationary[1],
                rhs=moving[0].bitcast(FP8X4),
                rhs_scale=moving[1],
                start=start,
                stop=stop,
            )

        x_codes, x_scales = {}, {}
        halves = [slice(half * HALF, (half + 1) * HALF) for half in range(2)]
        for s in range(PASSES):
            picked = held([P, S, PACK], BF16, f"picked{s}")
            words = picked[:].rearrange("p n j -> p (n j)").bitcast(I32).rearrange("p (n u) -> p n u", u=2)
            planes = held([P, 2, S], U32, f"planes{s}")
            for u in range(2):
                pairs = held([P, T, 2], BF16, f"pairs{s}{u}")
                cast(pairs, x_raw[s, u][:].rearrange("p e c -> p c e"), X_SCALAR[s, u])
                window = pairs[:].rearrange("p c e -> p (c e)").bitcast(U32)
                for nodes in halves if u == 1 else [slice(0, S)]:
                    entries = offs_t[:, nodes.start // 16 : nodes.stop // 16]
                    nc.vector.tensor_copy(planes[:, u, nodes], window.indirect(entries))
            for nodes in halves:
                nc.vector.tensor_copy(words[:, nodes], planes[:].bitcast(I32)[:, :, nodes].rearrange("p u n -> p n u"))
            x_codes[s] = held([P, S], U32, f"x_codes{s}")
            x_scales[s] = held([P, S], U8, f"x_scales{s}")
            for nodes in halves:
                quantise(x_codes[s][:, nodes], x_scales[s][:, nodes], picked[:, nodes, :].rearrange("p n j -> p (n j)"))

        spread = banks.tile([P, D, 2, P], F32, name=f"bank{2 * BLOCKS - 1}")
        gates = []
        for d in range(D):
            for i in range(2):
                nc.tensor.transpose(spread[:, d, i], gate_pairs[:, d, i : i + 1].to_broadcast([P, P]), identity[:])
        for d in range(D):
            gates.append(held([P, V], F32, f"gates{d}"))
            nc.scalar.activation(
                gates[d][:].rearrange("p (q i) -> p q i", i=2), spread[:, d].rearrange("p i q -> p q i"), COPY
            )

        idle = banks.tile([P, S], F32, name=f"bank{2 * BLOCKS - 1}")
        for i in range(WARM_PASSES):
            multiply(idle[:], (x_codes[1][:, S - P :], x_scales[1][:, S - P :]), (x_codes[0][:], x_scales[0][:]), True, True)

        w1_codes, w1_scales = {}, {}

        def prepare_w1(b, s, tiles_at_once):
            w1_codes[b, s] = held([P, PACK, P], U32, f"w1_codes{b}{s}")
            w1_scales[b, s] = held([P, PACK, P], U8, f"w1_scales{b}{s}")
            width = P // len(w1_raw[b, s])
            for c, raw in enumerate(w1_raw[b, s]):
                grouped = held([P, PACK, width, PACK], BF16, f"w1_grouped{b}{s}{c}")
                dst = grouped[:].rearrange("p t m (a e) -> p m a t e", e=2)
                src = raw.rearrange("p (a e) (m t) -> p m a t e", e=2, t=RUN)
                runs = src.shape[1]
                if (b, s) == (1, 0):
                    rest = runs - W1_SHORT
                    cast(dst[:, rest:], src[:, rest:], 0)
                    cast(dst[:, :rest], src[:, :rest], W1_SCALAR[b, s])
                elif (b, s) == (1, 1):
                    cast(dst, src, runs if c == 0 else 0)
                else:
                    cast(dst, src, W1_SCALAR[b, s])
                columns = slice(c * width, (c + 1) * width)
                for t in range(0, PACK, tiles_at_once):
                    some = slice(t, t + tiles_at_once)
                    quantise(
                        w1_codes[b, s][:, some, columns].rearrange("p t m -> p (t m)"),
                        w1_scales[b, s][:, some, columns].rearrange("p t m -> p (t m)"),
                        grouped[:, some].rearrange("p t m j -> p (t m j)"),
                    )

        acc, h = {}, {}

        def product1(b, s, nb):
            nodes = slice(nb * P, (nb + 1) * P)
            if s == 0:
                acc[b, nb] = banks.tile([P, PACK, P], F32, name=f"bank{b * BLOCKS + nb}")
            for t in range(PACK):
                multiply(
                    acc[b, nb][:, t, :],
                    (w1_codes[b, s][:, t, :], w1_scales[b, s][:, t, :]),
                    (x_codes[s][:, nodes], x_scales[s][:, nodes]),
                    s == 0 and t == 0,
                    s == PASSES - 1 and t == PACK - 1,
                )

        def last_pass_and_silu(b):
            for nb in range(BLOCKS):
                product1(b, PASSES - 1, nb)
                nc.scalar.activation(h[b, nb], acc[b, nb][:].rearrange("p t n -> p n t"), SILU)

        prepare_w1(0, 0, PACK)
        for nb in range(BLOCKS):
            product1(0, 0, nb)
        prepare_w1(0, 1, 2)
        prepare_w1(1, 0, PACK)
        h_first = [held([P, HALF, PACK], BF16, f"h_first{half}") for half in range(2)]
        for nb in range(BLOCKS):
            h[0, nb] = h_first[nb // 2][:, nb % 2 * P : (nb % 2 + 1) * P, :]
        last_pass_and_silu(0)
        for nb in range(BLOCKS):
            product1(1, 0, nb)
        prepare_w1(1, 1, 1)
        for nb in range(BLOCKS):
            h[1, nb] = held([P, P, PACK], BF16, f"h1{nb}")[:]
        last_pass_and_silu(1)

        h_codes = [held([P, S], U32, f"h_codes{s}") for s in range(PASSES)]
        h_scales = [held([P, S], U8, f"h_scales{s}") for s in range(PASSES)]
        w2_grouped, w2_operand = {}, {}

        def quantise_h(s, nodes, values):
            quantise(h_codes[s][:, nodes], h_scales[s][:, nodes], values.rearrange("p n t -> p (n t)"))

        def quantise_block(nb):
            quantise_h(1, slice(nb * P, (nb + 1) * P), h[1, nb])

        def cast_w2(s, first, count, cut):
            w2_grouped[s, first] = held([P, count * P, PACK], BF16, f"w2_grouped{s}{first}")
            dst = w2_grouped[s, first][:].rearrange("p (c i) (a e) -> p c a i e", i=RUN, e=2)
            cast(dst, w2_raw[s, first].rearrange("p (a e) (c i) -> p c a i e", i=RUN, e=2), cut)

        def quantise_w2(s, first, count):
            codes = held([P, count * P], U32, f"w2_codes{s}{first}")
            scales = held([P, count * P], U8, f"w2_scales{s}{first}")
            quantise(codes[:], scales[:], w2_grouped[s, first][:].rearrange("p c j -> p (c j)"))
            for i in range(count):
                w2_operand[s, first + i] = codes[:, i * P : (i + 1) * P], scales[:, i * P : (i + 1) * P]

        cast_w2(0, 0, 2, 0)
        quantise_h(0, halves[0], h_first[0][:])
        quantise_w2(0, 0, 2)
        cast_w2(1, 0, 2, 0)
        quantise_h(0, halves[1], h_first[1][:])
        quantise_w2(1, 0, 2)
        for nb in range(BLOCKS):
            quantise_block(nb)
        runs = P // RUN
        cast_w2(0, 2, 1, runs // 2)

        total, y = {}, {}

        def pass2(result, mt, s, nodes, last=True):
            moving = h_codes[s][:, nodes], h_scales[s][:, nodes]
            multiply(result, w2_operand[s, mt], moving, s == 0, s == 1 and last)

        def copy_y(mt):
            y[mt] = held([P, S], F32, f"y{mt}")
            nc.scalar.activation(y[mt][:], total[mt][:], COPY)

        everyone = slice(0, S)
        total[0] = [banks.tile([P, HALF], F32, name=f"bank{bank}") for bank in (0, 2 * BLOCKS - 2)]
        total[1] = banks.tile([P, S], F32, name="bank1")
        for half, nodes in enumerate(halves):
            pass2(total[0][half][:], 0, 0, nodes, last=False)
        pass2(total[1][:], 1, 0, everyone)
        for nb in range(BLOCKS):
            nodes = slice(nb * P, (nb + 1) * P)
            pass2(total[0][nb // 2][:, nb % 2 * P : (nb % 2 + 1) * P], 0, 1, nodes, last=nb % 2 == 1)
        pass2(total[1][:], 1, 1, everyone)
        y[0] = held([P, S], F32, "y0")
        for half, nodes in enumerate(halves):
            nc.scalar.activation(y[0][:, nodes], total[0][half][:], COPY)

        def quantise_and_multiply(mt, s):
            quantise_w2(s, mt, 1)
            if s == 0:
                total[mt] = banks.tile([P, S], F32, name=f"bank{mt}")
            pass2(total[mt][:], mt, s, everyone)

        cast_w2(0, 3, 1, 0)
        for mt in (2, 3):
            quantise_and_multiply(mt, 0)
        cast_w2(1, 2, 1, runs)
        copy_y(1)
        cast_w2(1, 3, 1, runs)

        out_rows = out.rearrange("(m p) v -> p m v", p=P)
        terms = {}

        def fetch(mt, d):
            terms[mt, d] = held([P, V], F32, f"terms{mt}{d}")
            nc.vector.tensor_tensor(terms[mt, d][:], y[mt][:].indirect(pos_t[d][:]), gates[d][:], MULT)

        def add_by_transposes(mt):
            turned = banks.tile([P, V], F32, name=f"bank{(2 * BLOCKS - 1, 2)[mt]}")
            for vb in range(V // P):
                targets = slice(vb * P, (vb + 1) * P)
                for d in range(D):
                    nc.tensor.matmul(
                        turned[:, targets],
                        terms[mt, d][:, targets],
                        identity[:],
                        start=(d == 0),
                        stop=(d == D - 1),
                        is_transpose=True,
                    )
            summed = held([P, V], F32, f"summed{mt}")
            nc.scalar.activation(summed[:], turned[:], COPY)
            back = banks.tile([P, V], F32, name=f"bank{(3, BLOCKS + 1)[mt]}")
            for vb in range(V // P):
                part = slice(vb * P, (vb + 1) * P)
                nc.tensor.transpose(back[:, part], summed[:, part], identity[:])
            result = held([P, V], F32, f"result{mt}")
            nc.scalar.activation(result[:], back[:], COPY)
            nc.scalar.dma_start(out=out_rows[:, mt, :], in_=result[:])

        fetch(0, 0)
        quantise_and_multiply(2, 1)
        fetch(0, 1)
        fetch(1, 0)
        quantise_and_multiply(3, 1)
        fetch(1, 1)
        copy_y(2)
        copy_y(3)
        for mt in range(TILES // 2):
            add_by_transposes(mt)
        def add_and_store(mt, targets, name):
            result = held([P, targets.stop - targets.start], F32, name)
            nc.vector.tensor_tensor(result[:], terms[mt, 0][:, targets], terms[mt, 1][:, targets], ADD)
            nc.sync.dma_start(out=out_rows[:, mt, targets], in_=result[:])

        parts = [slice(0, P), slice(P, V)]
        fetch(2, 0)
        fetch(2, 1)
        fetch(3, 0)
        terms[3, 1] = held([P, V], F32, "terms31")
        for i, targets in enumerate(parts):
            entries = pos_t[1][:, targets.start // 16 : targets.stop // 16]
            nc.vector.tensor_tensor(terms[3, 1][:, targets], y[3][:].indirect(entries), gates[1][:, targets], MULT)
            if i == 0:
                add_and_store(2, slice(0, V), "result2")
        for i, targets in enumerate(parts):
            add_and_store(3, targets, f"result3{i}")
